import numpy as np, ml_dtypes
CORES = [35,38,43,46]
N = 4
import mx_ref
BF = ml_dtypes.bfloat16
def gentries(a):
    return np.ascontiguousarray(a.reshape(8, 16, -1).transpose(0, 2, 1)).reshape(8, -1)
def gtable(e):
    e = np.asarray(e); return np.ascontiguousarray(e.reshape(8, -1, 16).transpose(0, 2, 1)).reshape(128, -1).astype(np.int32)
def gcols(t, e):
    v = np.concatenate([t.reshape(8, 16, -1, 4), np.zeros((8, 16, 1, 4), BF)], axis=2)
    return np.ascontiguousarray(np.stack([v[g][:, e[g]] for g in range(8)])).reshape(128, -1)
def tile(rs):
    return np.stack(rs, axis=2).reshape(128, -1).astype(BF)
def pick(q, e):
    c = np.concatenate([q[0].reshape(128, -1, 4), np.zeros((128, 1, 4), np.uint8)], axis=1); s = np.concatenate([q[1], np.ones((16, 1), np.uint8)], axis=1)
    return (np.ascontiguousarray(c[:, e].reshape(128, -1)), np.ascontiguousarray(s[:, e]))
def join(*qs):
    return (np.concatenate([q[0] for q in qs], axis=1), np.concatenate([q[1] for q in qs], axis=1))
def put(q, e, v):
    c, s = q[0].reshape(128, -1, 4).copy(), q[1].copy(); c[:, e] = v[0].reshape(128, -1, 4); s[:, e] = v[1]
    return (c.reshape(128, -1), s)
def pk(c, s):
    return (np.ascontiguousarray(c), mx_ref.live(s))
def emit(q):
    return q[0], q[1]
def packed(v, rng):
    q = [mx_ref.quantize(np.ascontiguousarray(v[r])) for r in range(N)]
    return np.stack([a for a, b in q]), np.stack([mx_ref.plane(b, rng) for a, b in q])
def values_of_codes():
    e, c = np.zeros((128, 128, 4), np.float32), np.zeros((128, 2, 4), np.uint8)
    e[np.arange(128), np.arange(128), 0] = 1
    c[:127, :, 0] = np.arange(256).reshape(2, 128).T[:127]
    return mx_ref.matmul(mx_ref.quantize(e.reshape(128, 512).astype(BF)), (c.reshape(128, 8), np.full((16, 2), 127, np.uint8))).T.reshape(-1).astype(np.float64)
CODE_VALUE, SCALE_VALUE = values_of_codes(), 2.0 ** (np.arange(256) - 127.0)
def decode(q):
    return (CODE_VALUE[q[0]].reshape(16, 8, -1, 4) * SCALE_VALUE[q[1]][:, None, :, None] + 0.0).reshape(128, -1).astype(np.float32)
def f(rng, *shape):
    return mx_ref.flush((rng.standard_normal(shape, dtype=np.float32) * np.exp2(rng.integers(-2, 3, shape[:-1] + (1,)))).astype(BF))
def wide(rng, *shape, cols=0):
    v = rng.standard_normal(shape, dtype=np.float32) * np.exp2(rng.integers(-12, 13, shape)).astype(np.float32)
    if cols: v *= np.repeat(np.exp2(rng.integers(-cols, cols + 1, shape[:-2] + (1, shape[-1] // 4))) * (rng.random(shape[:-2] + (1, shape[-1] // 4)) > 0.0625), 4, axis=-1).astype(np.float32)
    return mx_ref.flush(v.astype(BF))
C, H = 384, 192
STEP = [1, 2, 3]
def numbers_of(rng):
    return {"x": np.array(f(rng, N, 128, 4 * C)), "u": np.array(f(rng, N, 128, 512)), "v": np.array(f(rng, N, 128, 512))}
def lists(rng):
    e = np.tile(np.arange(C), (N, 8, 1))
    q = rng.permuted(e, axis=2)
    p = np.zeros((N, 8, C), np.int64)
    np.put_along_axis(p, q, np.ascontiguousarray(q.reshape(N, 8, H, 2)[..., ::-1]).reshape(N, 8, C), axis=2)
    return rng.permuted(e, axis=2), p
def stored(n, p):
    return {k: np.stack([gtable(e[r]) for r in range(N)]) for k, e in (("nx", n), ("iv", np.argsort(n, axis=2)), ("pr", p))}
def layer(rng, still=[]):
    w = np.array(f(rng, 128, 2048)).reshape(8, 16, 4, 8, 16, 4)
    for i in still:
        w[:, i] = 0
        w[:, :, :, :, i] = 0
    return w
def weights(rng, w):
    c, s = packed(np.stack([np.ascontiguousarray(w).reshape(128, 2048)] * N), rng)
    return {"wc": c, "ws": s}
def setup_inputs(rng):
    return {**numbers_of(rng), **stored(*lists(rng)), **weights(rng, layer(rng))}
def setup_inputs_ties(rng):
    d = numbers_of(rng)
    n, p = lists(rng)
    o = rng.permutation(N)
    k = rng.integers(-1, 2, (N, 8, C))
    k[o[1]] = 1
    k[o[2]] = 1
    t = rng.integers(0, 2, (8, C))
    t = np.where(np.arange(C) < p[o[3]], t, 1 - np.take_along_axis(t, p[o[3]], axis=1))
    k[o[3]] = np.where(t == 1, 1, rng.integers(-1, 1, (8, C)))
    a = np.exp2(rng.integers(-3, 4, (8, 1)).astype(np.float32))
    x = d["x"].reshape(N, 8, 16, C, 4)
    x[:, :, 0] = 0
    x[:, :, 0, :, 0] = k.astype(np.float32).astype(BF)
    x[:, :, 8:] = 0
    x[:, :, 8, :, 0] = (-1.125 * a).astype(BF)
    x[:, :, 10, :, 0] = (-0.0703125 * a).astype(BF)
    u = d["u"].reshape(N, 128, 128, 4)
    u[:, :, ::16] = 0
    for r in range(N):
        for h in range(0, 128, 16): u[r, h, h, 0] = 0.0 if r == o[0] else -1.0 if r == o[2] else 1.0
    w = layer(rng, [0])
    w[:, :, :, :, 8:] = 0
    for g in range(8):
        w[g, 8, 0, g, 8, 0] = -28.0
        for b in range(4): w[g, 10, b, g, 9, 0] = -2.0 ** (b - 5)
    return {"x": x.reshape(N, 128, 4 * C), "u": u.reshape(N, 128, 512), "v": d["v"], **stored(n, p), **weights(rng, w)}
def setup_inputs_near(rng):
    d = numbers_of(rng)
    k = np.where(rng.permutation(N) % 2 == 0, 2.0 ** -30, 1.0)
    x = rng.choice([-1.0, 1.0], (N, 8, 16, C, 4)) * (1.0 + 0.125 * rng.integers(0, 8, (N, 8, 16, C, 4))) * 64.0 * k[:, None, None, None, None]
    x[:, :, :9] = 0
    s = rng.integers(-1, 2, (N, 8, C)) * k[:, None, None]
    x[:, :, 0, :, 0] = 1.125 * s
    x[:, :, 1, :, 0] = -1.25 * s
    x[:, :, 7, :, 0] = k[:, None, None]
    x[:, :, 8, :, 0] = rng.choice([-1.0, 1.0], (N, 8, C)) * k[:, None, None]
    x[:, :, 9, :, 0] = 64.0 * k[:, None, None]
    for r in range(N):
        at = [0, C - 1, int(rng.integers(C)), int(rng.integers(C))]
        for g, j in zip(rng.permutation(8)[:4], at): x[r, g, 0, j, 0] = 2.0 ** 30 * rng.choice([-1.0, 1.0])
    u = d["u"].reshape(N, 128, 128, 4)
    u[:, :, ::16] = 0
    for h in range(0, 128, 16):
        u[:, h, h, 0] = (1.125 * k).astype(np.float32).astype(BF)
        u[:, h + 1, h, 0] = k.astype(np.float32).astype(BF)
        u[:, h + 2, h, 0] = k.astype(np.float32).astype(BF)
    w = layer(rng, list(range(10)))
    for g in range(8):
        w[g, 8, 0, g, 2, 0] = 2.0 ** -8
        w[g, 9, 0, g, 7, 0] = 1.0
    return {"x": x.astype(np.float32).reshape(N, 128, 4 * C).astype(BF), "u": u.reshape(N, 128, 512), "v": d["v"], **stored(*lists(rng)), **weights(rng, w)}
def setup_inputs_odd(rng):
    d = numbers_of(rng)
    x = (1.0 + (2 * rng.integers(0, 64, (N, 16, 8, C, 4)) + 1) * 2.0 ** -7) * np.exp2(-rng.integers(0, 7, (N, 16, 8, C, 4)).astype(np.float64)) * rng.choice([-1.0, 1.0], (N, 16, 8, C, 4))
    x[:, :, 0, :, 0] = rng.choice([1.96875, 1.875], (N, 16, C)) * 2.0 ** 8 * rng.choice([-1.0, 1.0], (N, 16, C))
    k = np.exp2(rng.integers(0, 4, (N, 8, C)) - 5.0)
    r = int(rng.integers(N))
    k[r] = k[r, :1].copy()
    x[:, ::2, 1, :, 0] = k * (1.0 + 0.125 * rng.integers(0, 2, (N, 8, C)))
    x[:, ::2, 2, :, 0] = k
    x[r, 0, 1, :, 0] = k[r, 0]
    u = d["u"].reshape(N, 16, 8, 128, 4)
    u[:, :, :, ::16] = 0
    for g in range(8):
        u[:, 2 * g, 1, 16 * g, 0] = 1.0
        u[:, 2 * g, 2, 16 * g, 0] = -1.0
    for g, i, e in ((0, 1, 4), (3, 2, 2)):
        u[r, :, :, 16 * g] = 0
        u[r, 0, i, 16 * g, 0] = 1.0
        u[r, 2 * e, 1, 16 * g, 0] = 1.875 * 2.0 ** -25
        u[r, 14, 2, 16 * g, 0] = -1.0
    return {"x": x.astype(np.float32).reshape(N, 128, 4 * C).astype(BF), "u": u.reshape(N, 128, 512), "v": d["v"], **stored(*lists(rng)), **weights(rng, layer(rng, [0, 1, 2, 8]))}
def setup_inputs_ends(rng):
    d = numbers_of(rng)
    o, e = rng.permutation(N) % 4, rng.permutation(N) % 4
    c = rng.choice([-1.0, 1.0], (N, C))
    c[:, H:] = -c[:, :H][:, ::-1]
    s = rng.choice([-1.0, 1.0], (N, 128, C, 4))
    s[o == 0] = -1
    s[o == 1] = c[o == 1][:, None, :, None]
    s[o == 3] = s[o == 3][:, :, :1]
    x = s * (0.63 + 0.06 * rng.random((N, 128, C, 4))) * 2.0 ** 30
    x[o == 3] = s[o == 3] * 2.0 ** -26
    x[o == 3, 48:64] = s[o == 3, 48:64] * 2.0 ** -30
    x[:, 120:] = s[:, 120:] * 2.0 ** -29
    a = np.stack([rng.permutation(8) % 2 * 2.0 - 1.0 for r in range(N)]) * np.where(o < 2, 2.0 ** 30, 2.0 ** -30)[:, None]
    u = d["u"].reshape(N, 128, 128, 4)
    u[:, :, ::16] = a.astype(np.float32).astype(BF)[:, None, :, None]
    v = rng.choice([-1.0, 1.0], (N, 128, 512)) * np.where(o % 2 == 0, 2.0 ** 30, 2.0 ** -30)[:, None, None]
    n, p = lists(rng)
    i = np.arange(C)
    p[o == 0] = i ^ 1
    p[o == 1] = C - 1 - i
    p[o == 2] = (i + H) % C
    n[e == 0] = i
    n[e == 1] = C - 1 - i
    n[e == 2] = (i + 1) % C
    n[e == 3] = p[e == 3]
    w = np.zeros((128, 4, 128, 4), np.float32)
    j = np.arange(128)
    for b in range(4): w[j, b, j, b] = np.where(j // 16 == 3, 0.0, np.where(j < 120, -4.0, 256.0))
    return {"x": x.astype(np.float32).reshape(N, 128, 4 * C).astype(BF), "u": u.reshape(N, 128, 512), "v": v.astype(np.float32).astype(BF), **stored(n, p), **weights(rng, w.astype(BF))}
def setup_inputs_spread(rng):
    d = setup_inputs(rng)
    d["x"] = wide(rng, N, 128, 4 * C, cols=6)
    return d
def check_inputs(d):
    b = []
    for k in ("x", "u", "v"):
        a = np.abs(d[k].astype(np.float32))
        if not (np.isfinite(a).all() and ((a == 0) | (a >= 2.0 ** -30) & (a <= 2.0 ** 30)).all()): b.append("a value of " + k)
    none, least, most = [emit(mx_ref.quantize(np.full((128, 16), k, np.float32).astype(BF)))[1][0, 0] for k in (0.0, 2.0 ** -8, 2.0 ** 8)]
    full = np.arange(C)
    for k in ("nx", "iv", "pr"):
        if not ((d[k] >= 0) & (d[k] < C)).all(): b.append("an entry of " + k)
    for r in range(N):
        n, i, p = [np.clip(gentries(d[k][r]), 0, C - 1) for k in ("nx", "iv", "pr")]
        if not (np.take_along_axis(i, n, axis=1) == full).all(): b.append("iv: not the inverse of nx")
        if not (np.take_along_axis(p, p, axis=1) == full).all() or (p == full).any(): b.append("pr: not pairs")
        if ((d["wc"][r] == 0x7F) | (d["wc"][r] == 0xFF)).any(): b.append("wc: a code that is no number")
        s = mx_ref.live(d["ws"][r])
        if ((s != none) & ((s < least) | (s > most))).any(): b.append("ws: a scale out of range")
        if (((d["wc"][r].reshape(16, 8, 512, 4) & 0x7F) != 0) & (s == none)[:, None, :, None]).any(): b.append("wc: a code other than zero under the scale of zeros")
        if (d["wc"][r] != d["wc"][0]).any() or (s != mx_ref.live(d["ws"][0])).any(): b.append("wc and ws: not the same on all ranks")
    return b
def reference(x, u, v, nx, iv, pr, wc, ws):
    qu = [mx_ref.quantize(u[r]) for r in range(N)]
    lay = [[pick(pk(wc[r], ws[r]), np.arange(128 * b, 128 * b + 128)) for b in range(4)] for r in range(N)]
    nxt, inv, pair = [[gentries(t[r]).astype(np.int64) for r in range(N)] for t in (nx, iv, pr)]
    now = [x[r] for r in range(N)]
    for step in STEP:
        had, made = [], []
        for r in range(N):
            n, m = nxt[r], inv[r]
            q = mx_ref.quantize(now[r])
            had.append(decode(q).astype(BF))
            bit = mx_ref.matmul(qu[r], q)[::16] > 0
            t = np.where(bit == np.take_along_axis(bit, pair[r], axis=1), pair[r], np.arange(C))
            for g in (0, 2, 4, 6, 1, 3, 5, 7):
                h = (g + 1) % 8
                w = n[g][t[g][m[g]]]
                n[g], m[g] = n[g][t[g]], t[g][m[g]]
                n[h], m[h] = n[h][w], w[m[h]]
            one = gcols(had[r], n).astype(np.float32)
            two = gcols(had[r], np.take_along_axis(n, n, axis=1)).astype(np.float32)
            z = mx_ref.quantize(((one + two) * np.float32(0.5)).astype(BF))
            made.append(mx_ref.quantize(tile([mx_ref.matmul(lay[r][b], z) * np.float32(0.03125) for b in range(4)])))
        for r in range(N):
            k = decode(join(pick(made[r], np.arange(H)), pick(made[r ^ step], np.arange(H, C)))).astype(BF)
            now[r] = (had[r].astype(np.float32) + gcols(k, inv[r]).astype(np.float32)).astype(BF)
    y, nl = np.zeros((N, 128, C), np.float32), np.zeros((N, 8, C), np.float32)
    oc, osc = np.zeros((N, 128, 4 * C), np.uint8), np.zeros((N, 16, C), np.uint8)
    for r in range(N):
        q = mx_ref.quantize(now[r])
        y[r] = mx_ref.matmul(mx_ref.quantize(v[r]), q)
        nl[r] = nxt[r]
        oc[r], osc[r] = emit(q)
    return {"y": y, "nl": nl, "oc": oc, "osc": osc}

@@ -1,0 +1,434 @@
+from concourse.mybir import dt, AluOpType, ActivationFunctionType
+
+C, HALF, NG = 384, 192, 24
+ROUNDS = 3
+STEPS = [1, 2, 3]
+ALU = AluOpType
+AF = ActivationFunctionType
+
+SCRATCH = {}
+
+
+def _sb(name, cols, dtype):
+    SCRATCH[name] = ("sbuf", [128, cols], dtype)
+
+
+def _mx(name, cols):
+    _sb("q" + name, cols, "float8_e4m3fn_x4")
+    _sb("s" + name, cols, "uint8")
+
+
+for _n, _c in (("x0", 4 * C), ("xt", 4 * C), ("ut", 512), ("vt", 512), ("ones", 515), ("et", 515), ("zh", 4 * HALF), ("zl", 4 * HALF),
+               ("hh", 4 * HALF), ("hl", 4 * HALF), ("fp", 4 * C), ("yp", 4 * C), ("kp", 4 * C),
+               ("ioc", C), ("mk", C), ("cb", 2 * C), ("ch", C), ("cq", 16), ("iv4b", 16),
+               ("by", C), ("by2", C), ("rmw", NG), ("fd", 4 * C), ("eb", 3 * C), ("scn", 3 * C), ("wm_", C), ("ws_", C), ("nti", 2 * C), ("nyw", 2 * C), ("tn", 2 * C),
+               ("nas", C), ("q1", C), ("uu", C), ("tx", C), ("tm", 2 * C), ("rm", C), ("rmp", C), ("rl", C)):
+    _sb(_n, _c, "bfloat16")
+for _n, _c in (("ia", NG), ("wa", NG), ("pmf", 1), ("hsub", 1), ("inv4", 1), ("odd", 1), ("ev", 1), ("oda", NG), ("hs", C), ("e1", NG), ("e2", NG),
+               ("e3", NG), ("e4", NG), ("lm", NG), ("ld", NG), ("lv", NG), ("hsubl", 1), ("nlf", C), ("yo", C), ("hsubc", 1), ("ptf", 32), ("ptt", 32)):
+    _sb(_n, _c, "float32")
+for _n, _c in (("it1", C), ("mk0", C), ("pt", 32), ("ip", 1), ("pm", 1), ("oi", 1), ("uo", 16), ("lists", 6 * NG)):
+    _sb(_n, _c, "int32")
+for _n, _c in (("uof", 16), ("wl", 6 * NG), ("offy", NG), ("offl", NG), ("offp", NG), ("offw", NG), ("wn", NG), ("wm", NG), ("ll", NG), ("wps", NG)):
+    _sb(_n, _c, "uint16")
+_mx("u", 128)
+_mx("u2", 256)
+_mx("v", 128)
+_mx("e", 512)
+_mx("w", 512)
+for _r in range(ROUNDS + 1):
+    _mx("t%d" % _r, C)
+for _r in range(ROUNDS):
+    for _n in ("zh", "zl", "hh", "hl", "ld"):
+        _mx("%s%d" % (_n, _r), HALF)
+SCRATCH["psa"] = ("psum", [128, 2048], "float32")
+SCRATCH["psb"] = ("psum", [128, 2048], "float32")
+
+DMA_GROUPS = ["x", "u", "v", "w", "la", "lb", "lp", "ly", "o"] + ["%s%d" % (n, r) for r in range(ROUNDS) for n in ("na", "rw", "sn", "sx", "sm", "sk", "sy")]
+SEMAPHORES = ["cv", "cs", "ct", "cg", "snd"] + ["d" + n for n in DMA_GROUPS] + ["arr%d" % r for r in range(ROUNDS)]
+
+PX, PY, MX, MY, NX, NY = [NG * k for k in range(6)]
+
+
+def W(name, a=0, b=None, step=1, p0=0, p1=128, ind=None):
+    return (name, a, SCRATCH[name][1][1] if b is None else b, step, p0, p1, ind)
+
+
+def rank_program(g, core, T, topo):
+    rank = T.rank_of(core)
+    if rank is None:
+        return
+
+    queues = {"v": g.vector, "s": g.scalar, "t": g.tensor, "g": g, "y": g.sync}
+    count, known, acc, snaps = {}, {q: {} for q in queues}, {}, {}
+
+    def ap(v, bits=None):
+        n, a, b, st, p0, p1, ind = v
+        rows = slice(None) if (p0, p1) == (0, 128) else slice(p0, p1)
+        t = T[n][rows, a:b] if st == 1 else T[n][rows, a:b:st]
+        if bits is not None:
+            t = t.bitcast(bits)
+        return t if ind is None else t.indirect(ap(ind))
+
+    def meets(r, s):
+        return r[1] < s[2] and s[1] < r[2] and r[4] < s[5] and s[4] < r[5]
+
+    def covers(r, s):
+        return r[3] == 1 and r[1] <= s[1] and s[2] <= r[2] and r[4] <= s[4] and s[5] <= r[5]
+
+    def whole(v):
+        if SCRATCH[v[0]][0] == "psum":
+            return (v[0], v[1] // 512 * 512, (v[2] + 511) // 512 * 512, 1, 0, 128, None)
+        return v
+
+    def phased(r, s):
+        return r[3] > 1 and r[3] == s[3] and (r[1] - s[1]) % r[3] != 0
+
+    def depend(q, reads, writes):
+        need = {}
+        for v, isw in [(whole(v), False) for v in reads] + [(whole(v), True) for v in writes]:
+            for (rv, rw, rq, sem, val) in acc.get(v[0], []):
+                if not (isw or rw) or not meets(v, rv) or phased(v, rv):
+                    continue
+                if not rw and rq == q and q != "y" and sem[0] == "c":
+                    continue
+                if rw and isw and rq == q and q == "t":
+                    continue
+                need[sem] = max(need.get(sem, 0), count[sem] if sem[0] == "d" else val)
+        k = known[q]
+        for sem in sorted(need, key=lambda m: (m[0] == "c", m)):
+            val = need[sem]
+            if k.get(sem, 0) >= val:
+                continue
+            queues[q].wait_ge(T.sem[sem], val)
+            k[sem] = val
+            for s2, v2 in snaps.get((sem, val), {}).items():
+                k[s2] = max(k.get(s2, 0), v2)
+
+    def note(q, reads, writes, sem, inc):
+        count[sem] = count.get(sem, 0) + inc
+        val = count[sem]
+        old = snaps.get((sem, val - inc), {}) if sem[0] == "d" else {}
+        new = dict(known[q])
+        for a, b in old.items():
+            new[a] = max(new.get(a, 0), b)
+        snaps[(sem, val)] = new
+        for v in [whole(v) for v in writes]:
+            lst = acc.setdefault(v[0], [])
+            lst[:] = [r for r in lst if not covers(v, r[0])]
+            lst.append((v, True, q, sem, val))
+        for v in [whole(v) for v in reads]:
+            acc.setdefault(v[0], []).append((v, False, q, sem, val))
+
+    def op(q, call, reads, writes, sem=None, inc=1):
+        reads = reads + [v[6] for v in reads + writes if v[6] is not None]
+        sem = sem or "c" + q
+        depend(q, reads, writes)
+        call(queues[q]).then_inc(T.sem[sem], inc)
+        note(q, reads, writes, sem, inc)
+
+    def dma(group, out, in_, q="y", bits=False):
+        o = ap(out, dt.uint8 if bits else None) if isinstance(out, tuple) else out
+        i = ap(in_, dt.uint8 if bits else None) if isinstance(in_, tuple) else in_
+        op(q, lambda e: e.dma_start(o, i), [in_] if isinstance(in_, tuple) else [], [out] if isinstance(out, tuple) else [], "d" + group, 16)
+
+    def ts(out, in0, s1, s2, o0, o1=None):
+        a1 = ap(s1) if isinstance(s1, tuple) else s1
+        a2 = ap(s2) if isinstance(s2, tuple) else s2
+        rd = [v for v in (in0, s1, s2) if isinstance(v, tuple)]
+        if o1 is None:
+            op("v", lambda e: e.tensor_scalar(ap(out), ap(in0), a1, None, o0), rd, [out])
+        else:
+            op("v", lambda e: e.tensor_scalar(ap(out), ap(in0), a1, a2, o0, o1), rd, [out])
+
+    def tt(out, in0, in1, o):
+        op("v", lambda e: e.tensor_tensor(ap(out), ap(in0), ap(in1), o), [in0, in1], [out])
+
+    def cp(out, in_):
+        op("v", lambda e: e.tensor_copy(ap(out), ap(in_)), [in_], [out])
+
+    def act(out, in_, func=AF.Copy, **kw):
+        op("s", lambda e: e.activation(ap(out), ap(in_), func, **kw), [in_], [out])
+
+    def scan(out, d0, d1, o0, o1):
+        op("v", lambda e: e.tensor_tensor_scan(ap(out), ap(d0), ap(d1), 0.0, o0, o1), [d0, d1], [out])
+
+    def quant(name, in_, a=0, b=None):
+        qo, so = W("q" + name, a, b), W("s" + name, a, b)
+        op("v", lambda e: e.quantize_mx(ap(qo), ap(so), ap(in_)), [in_], [qo, so])
+
+    def mm(out, ln, la, rn, ra, rb):
+        l, ls, r, rs = W("q" + ln, la, la + 128), W("s" + ln, la, la + 128), W("q" + rn, ra, rb), W("s" + rn, ra, rb)
+        op("t", lambda e: e.matmul_mx(ap(out), ap(l), ap(ls), ap(r), ap(rs), True, True), [l, ls, r, rs], [out])
+
+    def bank(n, k, w):
+        return W(n, 512 * k, 512 * k + w)
+
+    def wl(k):
+        return W("wl", k, k + NG)
+
+    def plane(n, b, a=0, w=C, ind=None):
+        return W(n, b * C + a, b * C + a + w, ind=ind)
+
+    def group(k):
+        return dict(p0=16 * (k % 8), p1=16 * (k % 8) + 16)
+
+    op("v", lambda e: e.memset(ap(W("lists", MX, MX + NG)), 0), [], [W("lists", MX, MX + NG)])
+    dma("x", W("x0"), T.x[:])
+    dma("u", W("ut"), T.u[:])
+    for grp, q, src, k in (("ly", "s", T.iv, MY), ("la", "s", T.pr, PX), ("la", "s", T.iv, MX), ("lb", "y", T.nx, NY), ("lb", "y", T.pr, PY), ("lb", "y", T.nx, NX)):
+        for o in range(1, 8, 2):
+            for to in (o, o + 1):
+                frm = o if k in (PX, MX, NX) else o - 1
+                if k != MX or to != o:
+                    dma(grp, W("lists", k, k + NG, **group(to)), src[16 * frm:16 * frm + 16, :], q=q)
+    op("y", lambda e: e.dma_start(T.qw[:, 0:512].bitcast(dt.uint8), T.wc[:]), [], [W("qw")], "dw", 16)
+    dma("w", W("sw"), T.ws[:])
+    dma("v", W("vt"), T.v[:])
+    op("v", lambda e: e.memset(ap(W("pt")), 0), [], [W("pt")])
+    for k in range(8):
+        frm = 16 * ((k - 1 + k % 2) % 8)
+        o = W("pt", 16 * (k % 2), 16 * (k % 2) + 16, 1, 32 * (k // 2), 32 * (k // 2) + 24)
+        dma("lp", o, T.pr[frm:frm + 16, :])
+
+    op("g", lambda e: e.iota(ap(W("ip")), [[1, 1]], 0, 1), [], [W("ip")])
+    op("g", lambda e: e.iota(ap(W("uo", 0, 8)), [[16, 8]], 112, 0), [], [W("uo", 0, 8)])
+    op("g", lambda e: e.iota(ap(W("ia")), [[16, NG]], 0, 0, allow_small_or_imprecise_dtypes=True), [], [W("ia")])
+    op("g", lambda e: e.iota(ap(W("it1")), [[1, C]], 128, -1), [], [W("it1")])
+    op("g", lambda e: e.iota(ap(W("ioc")), [[1, C]], -HALF, 0, allow_small_or_imprecise_dtypes=True), [], [W("ioc")])
+    ts(W("pm"), W("ip"), 15, None, ALU.bitwise_and)
+    op("v", lambda e: e.memset(ap(W("ones")), 1.0), [], [W("ones")])
+    op("g", lambda e: e.affine_select(ap(W("et")), ap(W("ones")), [[-1, 515]], ALU.is_equal, 0.0, 3, 4), [W("ones")], [W("et")])
+
+    def gcopy(out, in_):
+        op("g", lambda e: e.affine_select(ap(out), ap(in_), [[0, C]], ALU.is_gt, 0.0, 1, 0), [in_], [out])
+
+    for o in (W("tm", C, 2 * C), W("nti", 0, C), W("nas")):
+        gcopy(o, W("ioc"))
+    ts(W("oi"), W("ip"), 4, 1, ALU.logical_shift_right, ALU.bitwise_and)
+    cp(W("pmf"), W("pm"))
+    cp(W("odd"), W("oi"))
+    ts(W("ev"), W("odd"), -1.0, 1.0, ALU.mult, ALU.add)
+    ts(W("hsub"), W("pmf"), -512.0, 512.0 * 15 - HALF, ALU.mult, ALU.add)
+    ts(W("hsubc"), W("pmf"), -512.0, 512.0 * 15, ALU.mult, ALU.add)
+    ts(W("uo", 8, 16), W("uo", 0, 8), 96, None, ALU.bitwise_and)
+    cp(W("uof", 0, 8), W("uo", 8, 16))
+    ts(W("uof", 8, 16), W("uo", 8, 16), 16, None, ALU.add)
+    ts(W("wa"), W("ia"), W("pmf"), None, ALU.add)
+    ts(W("oda"), W("wa"), float(C), W("odd"), ALU.add, ALU.mult)
+    ts(W("mk0"), W("it1"), 15, None, ALU.bitwise_and)
+    ts(W("mk"), W("mk0"), 0.0, None, ALU.is_equal)
+    cp(wl(MY), W("lists", MY, MY + NG))
+    quant("u", W("ut"))
+    uoff = W("uof")
+    qs, qd = W("qu", ind=uoff), W("qu2")
+    op("v", lambda e: e.tensor_copy(ap(qd, dt.uint32), ap(qs, dt.uint32)), [qs], [qd])
+    ts(W("cb", 0, C), W("mk"), -4.0, 4.0, ALU.mult, ALU.add)
+    gcopy(W("cb", C, 2 * C), W("cb", 0, C))
+    ts(W("ch"), W("mk"), -16896.0, 512.0, ALU.mult, ALU.add)
+    ts(W("cq"), W("mk", 0, 16), -0.25, 0.25, ALU.mult, ALU.add)
+    scan(W("iv4b"), W("cq"), W("mk", 0, 16), ALU.mult, ALU.add)
+    cp(W("inv4"), W("iv4b", 15, 16))
+    ts(W("hsubl"), W("ev"), -float(C), W("hsub"), ALU.mult, ALU.add)
+
+    def hold(row):
+        scan(W("hs"), W("ch"), row, ALU.add, ALU.max)
+        return W("hs", 15, C, 16)
+
+    def masked(out, row):
+        tt(W("wm_"), row, W("mk"), ALU.mult)
+        scan(W("ws_"), W("cb", 0, C), W("wm_"), ALU.mult, ALU.add)
+        ts(out, W("ws_", 15, C, 16), W("inv4"), float(HALF), ALU.mult, ALU.add)
+
+    def ahead_n2():
+        act(W("tn", 0, C), W("tx", ind=wl(NY)))
+        act(W("tn", C, 2 * C), W("tn", 0, C, ind=wl(PY)))
+
+    def ahead_m(r):
+        if r == 0:
+            act(W("rmp"), W("tm", 0, C, ind=wl(PX)))
+        act(W("rl"), W("tm", ind=wl(MX)))
+        if r > 0:
+            act(W("rmp"), W("tm", 0, C, ind=W("wps")))
+            op("y", lambda e: e.dma_start(T.rmw[:], T.rmp[0:128:16, :]), [W("rmp")], [W("rmw")], "drw%d" % r, 16)
+
+    def ahead_w(r):
+        ts(W("lm"), wl(MY), float(HALF), None, ALU.subtract)
+        if r == 0:
+            ts(W("lv"), hold(W("rmp")), W("hsubc"), None, ALU.subtract)
+            tt(W("ld"), W("lv"), W("lm"), ALU.subtract)
+        ts(W("ll"), hold(W("rl")), W("hsubl"), None, ALU.subtract)
+
+    cp(wl(PX), W("lists", PX, PX + NG))
+    act(W("tm", 0, C), W("ioc", ind=wl(MY)))
+    act(W("su2"), W("su", ind=uoff))
+    ts(W("e1"), W("lists", MX, MX + NG), W("ev"), None, ALU.mult)
+    tt(W("e2"), W("e1"), W("oda"), ALU.add)
+    cp(wl(MX), W("e2"))
+    ahead_m(0)
+    quant("t0", W("x0", 0, 4 * HALF), 0, HALF)
+    quant("t0", W("x0", 4 * HALF, 4 * C), HALF, C)
+    cp(W("wl", 4 * NG, 6 * NG), W("lists", 4 * NG, 6 * NG))
+    cp(W("nyw", 0, C), W("ioc", ind=wl(NY)))
+    cp(wl(PY), W("lists", PY, PY + NG))
+    cp(W("tx"), W("ioc", ind=wl(NX)))
+    for b in range(4):
+        quant("e", W("et", 3 - b, 515 - b), 128 * b, 128 * b + 128)
+    ahead_w(0)
+
+    for r, step in enumerate(STEPS):
+        last = r == ROUNDS - 1
+        t = "t%d" % r
+        partner = T.cores[rank ^ step]
+        mm(bank("psb", 0, HALF), "u2", 0, t, 0, HALF)
+        mm(bank("psb", 1, HALF), "u2", 0, t, HALF, C)
+        mm(bank("psb", 2, C), "u2", 128, t, 0, C)
+        act(W("by", 0, HALF), bank("psb", 0, HALF), AF.Sign, bias=-2.0 ** -100)
+        act(W("by", HALF, C), bank("psb", 1, HALF), AF.Sign, bias=-2.0 ** -100)
+        if r == 0:
+            act(W("nyw", C, 2 * C), W("nyw", 0, C, ind=wl(PY)))
+            ahead_n2()
+        act(W("eb", C, 2 * C), bank("psb", 2, C), AF.Sign, bias=-2.0 ** -100)
+        act(W("eb", 2 * C, 3 * C), W("eb", C, 2 * C, ind=wl(PX)))
+        cp(W("by2"), W("by"))
+        tt(W("eb", 0, C), W("by", ind=wl(PY)), W("by2"), ALU.mult)
+        scan(W("scn", 0, C), W("cb", 0, C), W("eb", 0, C), ALU.mult, ALU.add)
+        ts(W("e1"), W("scn", 15, C, 16), 0.0, float(C), ALU.is_gt, ALU.mult)
+        tt(W("e2"), W("e1"), W("wa"), ALU.add)
+        cp(W("offy"), W("e2"))
+        for b in range(4):
+            mm(bank("psa", b, C), "e", 128 * b, t, 0, C)
+        act(W("nti", C, 2 * C), W("nyw", ind=W("offy")))
+        act(W("q1"), W("tn", ind=W("offy")))
+        for k in range(0, 8, 2):
+            dma("na%d" % r, W("nas", **group(k)), W("nti", C, 2 * C, **group(k + 1)))
+        scan(W("scn", C, 3 * C), W("cb"), W("eb", C, 3 * C), ALU.mult, ALU.add)
+        tt(W("e1"), W("scn", C + 15, 2 * C, 16), W("scn", 2 * C + 15, 3 * C, 16), ALU.mult)
+        ts(W("e2"), W("e1"), 0.0, None, ALU.is_gt)
+        if r > 0:
+            tt(W("ld"), W("rmw"), W("lm"), ALU.subtract)
+        tt(W("e3"), W("e2"), W("ld"), ALU.mult)
+        tt(W("e4"), W("e3"), W("lm"), ALU.add)
+        ts(W("offl"), W("e4"), float(HALF), None, ALU.add)
+        act(W("uu"), W("q1", ind=W("offl")))
+        masked(W("offp"), W("nti", ind=W("ll")))
+        act(plane("fp", 0), bank("psa", 0, C))
+        gcopy(plane("fd", 0), plane("fp", 0))
+        masked(W("offw"), W("uu", ind=W("offp")))
+        for b in range(1, 4):
+            act(plane("fp", b), bank("psa", b, C))
+        gcopy(plane("fd", 1), plane("fp", 1))
+        if last:
+            act(W("nlf"), W("nas", ind=W("offw")), AF.Identity, bias=float(HALF))
+        else:
+            act(W("tx"), W("nas", ind=W("offw")))
+        masked(W("wn"), W("nas", ind=W("offw")))
+        if not last:
+            for o in range(1, 8, 2):
+                for to in (o, o + 1):
+                    dma("sn%d" % r, W("nyw", 0, C, **group(to)), W("tx", **group(o - 1)))
+                    dma("sn%d" % r, W("wl", NY, NY + NG, **group(to)), W("wn", **group(o - 1)))
+            for o in range(1, 8, 2):
+                dma("sx%d" % r, W("tx", **group(o + 1)), W("tx", **group(o)))
+        hi, lo = W("wn", 12, 24), W("wn", 0, 12)
+        for b in (3, 2):
+            act(plane("kp", b), plane("fp", b, ind=W("wn")))
+        for b in (0, 1):
+            tt(plane("yp", b), plane("fp", b, ind=W("wn")), plane("fd", b), ALU.add)
+        for b in (3, 2):
+            tt(plane("yp", b), bank("psa", b, C), plane("kp", b), ALU.add)
+        for b in (0, 1, 2):
+            act(W("zh", b, 4 * HALF, 4), plane("yp", b, ind=hi), scale=0.5)
+        ts(W("zh", 3, 4 * HALF, 4), plane("yp", 3, ind=hi), 0.5, None, ALU.mult)
+        zh, zl, hh, hl, ld = ["%s%d" % (n, r) for n in ("zh", "zl", "hh", "hl", "ld")]
+        quant(zh, W("zh"))
+        for b in (0, 1):
+            act(W("zl", b, 4 * HALF, 4), plane("yp", b, ind=lo), scale=0.5)
+        ts(W("zl", 2, 4 * HALF, 4), plane("yp", 2, ind=lo), 0.5, None, ALU.mult)
+        for b in range(4):
+            mm(bank("psb", b, HALF), "w", 128 * b, zh, 0, HALF)
+        for b in range(4):
+            if b % 2 == 0:
+                ts(W("hh", b, 4 * HALF, 4), bank("psb", b, HALF), 0.03125, None, ALU.mult)
+            else:
+                act(W("hh", b, 4 * HALF, 4), bank("psb", b, HALF), scale=0.03125)
+        quant(hh, W("hh"))
+        act(W("zl", 3, 4 * HALF, 4), plane("yp", 3, ind=lo), scale=0.5)
+        quant(zl, W("zl"))
+        for b in range(4):
+            mm(bank("psa", b, HALF), "w", 128 * b, zl, 0, HALF)
+        rid, pid = topo.addr(partner)[:2]
+        mask = topo.mask(core, partner)
+        arr = "arr%d" % r
+        depend("g", [W("q" + hh), W("s" + hh)], [])
+        g.remote_dma(T["q" + ld][:, 0:HALF].bitcast(dt.uint8), T["q" + hh][:, 0:HALF].bitcast(dt.uint8), T.sem[arr], T.sem.snd, pid, rid, mask)
+        g.remote_dma(T["s" + ld][:, 0:HALF], T["s" + hh][:, 0:HALF], T.sem[arr], T.sem.snd, pid, rid, mask)
+        count["snd"] = count.get("snd", 0) + 2 * len(topo.engines(core, partner))
+        count[arr] = 2 * len(topo.engines(partner, core))
+        for nm in ("q" + ld, "s" + ld):
+            acc.setdefault(nm, []).append((W(nm), True, "far", arr, count[arr]))
+        for b in range(4):
+            act(W("hl", b, 4 * HALF, 4), bank("psa", b, HALF), scale=0.03125)
+        if not last:
+            ahead_n2()
+        sc = W("rm", ind=W("wn"))
+        op("v", lambda e: e.tensor_copy(ap(sc), ap(W("ioc"))), [W("ioc")], [sc])
+        quant(hl, W("hl"))
+        ts(W("wm"), hold(W("rm")), W("hsub"), None, ALU.subtract)
+        if r == 0:
+            cp(W("ptf"), W("pt"))
+            op("v", lambda e: e.transpose(ap(W("ptt")), ap(W("ptf"))), [W("ptf")], [W("ptt")])
+            cp(W("wps"), W("ptt", 0, NG))
+            quant("v", W("vt"))
+        if not last:
+            cp(W("nyw", C, 2 * C), W("nyw", 0, C, ind=wl(PY)))
+        for b in range(4):
+            mm(bank("psb", b, HALF), "e", 128 * b, hl, 0, HALF)
+        for b in range(4):
+            if b % 2 == 0:
+                cp(plane("kp", b, 0, HALF), bank("psb", b, HALF))
+            else:
+                act(plane("kp", b, 0, HALF), bank("psb", b, HALF))
+        if not last:
+            for o in range(1, 8, 2):
+                for to in (o, o + 1):
+                    dma("sm%d" % r, W("tm", 0, C, **group(to)), W("rm", **group(o - 1)))
+            for o in range(1, 8, 2):
+                dma("sk%d" % r, W("wl", MX, MX + NG, **group(o + 1)), W("wm", **group(o)))
+            for o in range(1, 8, 2):
+                for to in (o, o + 1):
+                    dma("sy%d" % r, W("wl", MY, MY + NG, **group(to)), W("wm", **group(o - 1)))
+        else:
+            op("y", lambda e: e.dma_start(T.nl[:], T.nlf[0:128:16, :]), [W("nlf")], [], "do", 16)
+        for b in (3, 0, 1, 2):
+            mm(bank("psa", b, HALF), "e", 128 * b, ld, 0, HALF)
+        for b in (3, 2):
+            mm(bank("psb", b, C), "e", 128 * b, t, 0, C)
+        act(plane("kp", 3, HALF, HALF), bank("psa", 3, HALF))
+        cp(plane("kp", 0, HALF, HALF), bank("psa", 0, HALF))
+        act(plane("yp", 3), plane("kp", 3, ind=W("wm")))
+        for b in (1, 2):
+            act(plane("kp", b, HALF, HALF), bank("psa", b, HALF))
+        act(plane("yp", 2), plane("kp", 2, ind=W("wm")))
+        for b in (0, 1):
+            tt(W("xt", b, 4 * C, 4), plane("kp", b, ind=W("wm")), plane("fp", b), ALU.add)
+        for b in (3, 2):
+            tt(W("xt", b, 4 * C, 4), bank("psb", b, C), plane("yp", b), ALU.add)
+        quant("t%d" % (r + 1), W("xt", 0, 4 * HALF), 0, HALF)
+        quant("t%d" % (r + 1), W("xt", 4 * HALF, 4 * C), HALF, C)
+        if not last:
+            ahead_m(r + 1)
+            ahead_w(r + 1)
+
+    f = "t%d" % ROUNDS
+    mm(bank("psb", 0, HALF), "v", 0, f, 0, HALF)
+    mm(bank("psb", 1, HALF), "v", 0, f, HALF, C)
+    op("s", lambda e: e.dma_start(T.oc[:], T["q" + f][:, 0:C].bitcast(dt.uint8)), [W("q" + f)], [], "do", 16)
+    for k in range(4):
+        op("y", lambda e: e.dma_start(T.osc[4 * k:4 * k + 4, :], T["s" + f][32 * k:32 * k + 4, 0:C]), [W("s" + f)], [], "do", 16)
+    cp(W("yo", 0, HALF), bank("psb", 0, HALF))
+    act(W("yo", HALF, C), bank("psb", 1, HALF))
+    dma("o", T.y[:, 0:HALF], W("yo", 0, HALF))
+    dma("o", T.y[:, HALF:C], W("yo", HALF, C), q="s")
+    for sem in sorted(count):
+        g.wait_ge(T.sem[sem], count[sem])

@@ -3,8 +3,10 @@ from concourse.mybir import dt, AluOpType, ActivationFunctionType
 C, HALF, NG = 384, 192, 24
 ROUNDS = 3
 STEPS = [1, 2, 3]
+BIG = 2.0 ** 40
 ALU = AluOpType
 AF = ActivationFunctionType
+SPLIT = True
 
 SCRATCH = {}
 
@@ -18,36 +20,36 @@ def _mx(name, cols):
     _sb("s" + name, cols, "uint8")
 
 
-for _n, _c in (("x0", 4 * C), ("xt", 4 * C), ("ut", 512), ("vt", 512), ("ones", 515), ("et", 515), ("zh", 4 * HALF), ("zl", 4 * HALF),
-               ("hh", 4 * HALF), ("hl", 4 * HALF), ("fp", 4 * C), ("yp", 4 * C), ("kp", 4 * C),
-               ("ioc", C), ("mk", C), ("cb", 2 * C), ("ch", C), ("cq", 16), ("iv4b", 16),
-               ("by", C), ("by2", C), ("rmw", NG), ("fd", 4 * C), ("eb", 3 * C), ("scn", 3 * C), ("wm_", C), ("ws_", C), ("nti", 2 * C), ("nyw", 2 * C), ("tn", 2 * C),
-               ("nas", C), ("q1", C), ("uu", C), ("tx", C), ("tm", 2 * C), ("rm", C), ("rmp", C), ("rl", C)):
+for _n, _c in (("x0", 4 * C), ("xt", 4 * C), ("ut", 512), ("vt", 512), ("half", 515), ("et", 515), ("zt", 4 * C), ("hh", 4 * HALF), ("hl", 4 * HALF),
+               ("fp", 4 * C), ("an", 4 * C), ("xn", 4 * C), ("ioc", C), ("hk", C), ("hk16", 16), ("sg", 2 * C), ("scn", 4 * C),
+               ("nw", C), ("nti", C), ("qb", 2 * C), ("q2", C), ("p4", C), ("uu", C), ("wr", C), ("nas", C), ("nb", 2 * C + HALF), ("rm", C)):
     _sb(_n, _c, "bfloat16")
-for _n, _c in (("ia", NG), ("wa", NG), ("pmf", 1), ("hsub", 1), ("inv4", 1), ("odd", 1), ("ev", 1), ("oda", NG), ("hs", C), ("e1", NG), ("e2", NG),
-               ("e3", NG), ("e4", NG), ("lm", NG), ("ld", NG), ("lv", NG), ("hsubl", 1), ("nlf", C), ("yo", C), ("hsubc", 1), ("ptf", 32), ("ptt", 32)):
+for _n, _c in (("ia", NG), ("wa", NG), ("j16", 16), ("ja", 16), ("jb", 16), ("pmf", 1), ("kinv", 1), ("kin2", 1), ("mid", NG), ("dlt", NG),
+               ("e1", NG), ("e2", NG), ("e3", NG), ("nlf", C), ("yo", C)):
     _sb(_n, _c, "float32")
-for _n, _c in (("it1", C), ("mk0", C), ("pt", 32), ("ip", 1), ("pm", 1), ("oi", 1), ("uo", 16), ("lists", 6 * NG)):
+for _n, _c in (("ip", 1), ("pm", 1), ("uo", 16), ("lists", 5 * NG)):
     _sb(_n, _c, "int32")
-for _n, _c in (("uof", 16), ("wl", 6 * NG), ("offy", NG), ("offl", NG), ("offp", NG), ("offw", NG), ("wn", NG), ("wm", NG), ("ll", NG), ("wps", NG)):
+for _n, _c in (("uof", 8), ("rep", NG), ("wl", 5 * NG), ("ta", NG), ("tb", NG), ("ll", NG), ("rw", NG), ("wp", NG), ("ww", NG), ("wn", 2 * NG + 12), ("wm", NG)):
     _sb(_n, _c, "uint16")
 _mx("u", 128)
-_mx("u2", 256)
+_mx("u2", 128)
 _mx("v", 128)
 _mx("e", 512)
 _mx("w", 512)
 for _r in range(ROUNDS + 1):
     _mx("t%d" % _r, C)
 for _r in range(ROUNDS):
-    for _n in ("zh", "zl", "hh", "hl", "ld"):
-        _mx("%s%d" % (_n, _r), HALF)
+    _mx("z%d" % _r, C)
+    _mx("hh%d" % _r, HALF)
+    _mx("k%d" % _r, C)
 SCRATCH["psa"] = ("psum", [128, 2048], "float32")
 SCRATCH["psb"] = ("psum", [128, 2048], "float32")
 
-DMA_GROUPS = ["x", "u", "v", "w", "la", "lb", "lp", "ly", "o"] + ["%s%d" % (n, r) for r in range(ROUNDS) for n in ("na", "rw", "sn", "sx", "sm", "sk", "sy")]
+DMA_GROUPS = ["x", "u", "v", "w", "la", "lb", "lc", "ld", "o"] + ["%s%d" % (n, r) for r in range(ROUNDS) for n in ("sw", "na", "n", "m", "mw", "ll", "tn")]
 SEMAPHORES = ["cv", "cs", "ct", "cg", "snd"] + ["d" + n for n in DMA_GROUPS] + ["arr%d" % r for r in range(ROUNDS)]
 
-PX, PY, MX, MY, NX, NY = [NG * k for k in range(6)]
+PR, TW, OF, NW, MQ = [NG * k for k in range(5)]
+EVEN, ODD = range(0, 8, 2), range(1, 8, 2)
 
 
 def W(name, a=0, b=None, step=1, p0=0, p1=128, ind=None):
@@ -90,7 +92,7 @@ def rank_program(g, core, T, topo):
             for (rv, rw, rq, sem, val) in acc.get(v[0], []):
                 if not (isw or rw) or not meets(v, rv) or phased(v, rv):
                     continue
-                if not rw and rq == q and q != "y" and sem[0] == "c":
+                if not rw and rq == q and q == "t":
                     continue
                 if rw and isw and rq == q and q == "t":
                     continue
@@ -127,9 +129,9 @@ def rank_program(g, core, T, topo):
         call(queues[q]).then_inc(T.sem[sem], inc)
         note(q, reads, writes, sem, inc)
 
-    def dma(group, out, in_, q="y", bits=False):
-        o = ap(out, dt.uint8 if bits else None) if isinstance(out, tuple) else out
-        i = ap(in_, dt.uint8 if bits else None) if isinstance(in_, tuple) else in_
+    def dma(group, out, in_, q="y"):
+        o = ap(out) if isinstance(out, tuple) else out
+        i = ap(in_) if isinstance(in_, tuple) else in_
         op(q, lambda e: e.dma_start(o, i), [in_] if isinstance(in_, tuple) else [], [out] if isinstance(out, tuple) else [], "d" + group, 16)
 
     def ts(out, in0, s1, s2, o0, o1=None):
@@ -150,8 +152,20 @@ def rank_program(g, core, T, topo):
     def act(out, in_, func=AF.Copy, **kw):
         op("s", lambda e: e.activation(ap(out), ap(in_), func, **kw), [in_], [out])
 
-    def scan(out, d0, d1, o0, o1):
-        op("v", lambda e: e.tensor_tensor_scan(ap(out), ap(d0), ap(d1), 0.0, o0, o1), [d0, d1], [out])
+    def move(q, out, in_, scale=None):
+        if q == "s":
+            act(out, in_) if scale is None else act(out, in_, scale=scale)
+        elif scale is None:
+            cp(out, in_)
+        else:
+            ts(out, in_, scale, None, ALU.mult)
+
+    def scan(out, d0, d1, first, o0, o1):
+        op("v", lambda e: e.tensor_tensor_scan(ap(out), ap(d0), ap(d1), first, o0, o1), [d0, d1], [out])
+
+    def iota(out, pattern, base, mult):
+        kw = {} if SCRATCH[out[0]][2] == "int32" else {"allow_small_or_imprecise_dtypes": True}
+        op("g", lambda e: e.iota(ap(out), pattern, base, mult, **kw), [], [out])
 
     def quant(name, in_, a=0, b=None):
         qo, so = W("q" + name, a, b), W("s" + name, a, b)
@@ -170,262 +184,219 @@ def rank_program(g, core, T, topo):
     def plane(n, b, a=0, w=C, ind=None):
         return W(n, b * C + a, b * C + a + w, ind=ind)
 
-    def group(k):
-        return dict(p0=16 * (k % 8), p1=16 * (k % 8) + 16)
+    def part(v, k):
+        return v[:4] + (16 * (k % 8), 16 * (k % 8) + 16, None)
 
-    op("v", lambda e: e.memset(ap(W("lists", MX, MX + NG)), 0), [], [W("lists", MX, MX + NG)])
+    def shift(grp, out, in_, to, by):
+        for k in to:
+            dma(grp, part(out, k), part(in_, k + by))
+
+    turn = [0]
+
+    def hold(row):
+        n, at = row[2] - row[1], C * (turn[0] % 4)
+        turn[0] += 1
+        scan(W("scn", at, at + n), W("hk", 0, n), row, 0.0, ALU.mult, ALU.add)
+        return W("scn", at + 15, at + n, 16)
+
+    def wrap(out, row):
+        ts(out, hold(row), W("kinv"), float(HALF), ALU.mult, ALU.add)
+
     dma("x", W("x0"), T.x[:])
-    dma("u", W("ut"), T.u[:])
-    for grp, q, src, k in (("ly", "s", T.iv, MY), ("la", "s", T.pr, PX), ("la", "s", T.iv, MX), ("lb", "y", T.nx, NY), ("lb", "y", T.pr, PY), ("lb", "y", T.nx, NX)):
-        for o in range(1, 8, 2):
-            for to in (o, o + 1):
-                frm = o if k in (PX, MX, NX) else o - 1
-                if k != MX or to != o:
-                    dma(grp, W("lists", k, k + NG, **group(to)), src[16 * frm:16 * frm + 16, :], q=q)
+    dma("u", W("ut"), T.u[:], q="s")
+    for grp, q, k, odd, even in (("la", "s", TW, (T.nx, 0), (T.iv, -2)), ("lb", "y", OF, (T.nx, -1), (T.iv, -1)),
+                                 ("lb", "y", PR, (T.pr, 0), (T.pr, -2)), ("lc", "s", NW, (T.iv, -1), (T.nx, -2))):
+        for to in range(8):
+            src, by = odd if to % 2 else even
+            frm = 16 * ((to + by) % 8)
+            dma(grp, part(W("lists", k, k + NG), to), src[frm:frm + 16, :], q=q)
+
+    iota(W("ip"), [[1, 1]], 0, 1)
+    iota(W("j16"), [[1, 16]], 0, 0)
+    iota(W("ia"), [[16, NG]], 0, 0)
+    iota(W("uo", 0, 8), [[32, 4], [-80, 2]], 96, 0)
+    op("v", lambda e: e.memset(ap(W("half")), 0.5), [], [W("half")])
+    op("g", lambda e: e.affine_select(ap(W("et")), ap(W("half")), [[-1, 515]], ALU.is_equal, 0.0, 3, 4), [W("half")], [W("et")])
+    ts(W("pm"), W("ip"), 15, None, ALU.bitwise_and)
+    scan(W("ioc"), W("half", 0, C), W("half", 0, C), -HALF - 1.0, ALU.add, ALU.add)
+    cp(W("pmf"), W("pm"))
+    ts(W("uo", 8, 16), W("uo", 0, 8), 127, None, ALU.bitwise_and)
+    ts(W("wa"), W("ia"), W("pmf"), None, ALU.add)
+    ts(W("ja"), W("j16"), W("pmf"), None, ALU.subtract)
+    cp(W("uof"), W("uo", 8, 16))
+    ts(W("lists", MQ, MQ + NG), W("wa"), float(C), None, ALU.add)
+    ts(W("jb"), W("ja"), 1.0, BIG, ALU.is_equal, ALU.mult)
+    ts(W("j16"), W("ja"), 0.0, None, ALU.is_gt)
+    ts(W("rep"), W("ia"), 0.0, W("pmf"), ALU.mult, ALU.add)
+    tt(W("hk16"), W("j16"), W("jb"), ALU.max)
+    ts(W("kinv"), W("pmf"), 15.0, 1.0 / BIG, ALU.is_equal, ALU.max)
+    ts(W("kin2"), W("pmf"), 15.0, 1.0 / BIG / BIG, ALU.is_equal, ALU.max)
+    cp(W("ll"), W("wa"))
+    for to in EVEN:
+        frm = 16 * ((to - 2) % 8)
+        dma("ld", part(W("lists", MQ, MQ + NG), to), T.iv[frm:frm + 16, :])
     op("y", lambda e: e.dma_start(T.qw[:, 0:512].bitcast(dt.uint8), T.wc[:]), [], [W("qw")], "dw", 16)
     dma("w", W("sw"), T.ws[:])
     dma("v", W("vt"), T.v[:])
-    op("v", lambda e: e.memset(ap(W("pt")), 0), [], [W("pt")])
-    for k in range(8):
-        frm = 16 * ((k - 1 + k % 2) % 8)
-        o = W("pt", 16 * (k % 2), 16 * (k % 2) + 16, 1, 32 * (k // 2), 32 * (k // 2) + 24)
-        dma("lp", o, T.pr[frm:frm + 16, :])
+    act(W("hk"), W("hk16", ind=W("rep")))
+    cp(W("nas"), W("ioc"))
 
-    op("g", lambda e: e.iota(ap(W("ip")), [[1, 1]], 0, 1), [], [W("ip")])
-    op("g", lambda e: e.iota(ap(W("uo", 0, 8)), [[16, 8]], 112, 0), [], [W("uo", 0, 8)])
-    op("g", lambda e: e.iota(ap(W("ia")), [[16, NG]], 0, 0, allow_small_or_imprecise_dtypes=True), [], [W("ia")])
-    op("g", lambda e: e.iota(ap(W("it1")), [[1, C]], 128, -1), [], [W("it1")])
-    op("g", lambda e: e.iota(ap(W("ioc")), [[1, C]], -HALF, 0, allow_small_or_imprecise_dtypes=True), [], [W("ioc")])
-    ts(W("pm"), W("ip"), 15, None, ALU.bitwise_and)
-    op("v", lambda e: e.memset(ap(W("ones")), 1.0), [], [W("ones")])
-    op("g", lambda e: e.affine_select(ap(W("et")), ap(W("ones")), [[-1, 515]], ALU.is_equal, 0.0, 3, 4), [W("ones")], [W("et")])
+    nrow, nw_, tn = W("nb", HALF, HALF + C), W("wn", 12, 36), W("qb", C, 2 * C)
 
-    def gcopy(out, in_):
-        op("g", lambda e: e.affine_select(ap(out), ap(in_), [[0, C]], ALU.is_gt, 0.0, 1, 0), [in_], [out])
+    def ahead():
+        act(tn, nrow[:6] + (wl(OF),))
 
-    for o in (W("tm", C, 2 * C), W("nti", 0, C), W("nas")):
-        gcopy(o, W("ioc"))
-    ts(W("oi"), W("ip"), 4, 1, ALU.logical_shift_right, ALU.bitwise_and)
-    cp(W("pmf"), W("pm"))
-    cp(W("odd"), W("oi"))
-    ts(W("ev"), W("odd"), -1.0, 1.0, ALU.mult, ALU.add)
-    ts(W("hsub"), W("pmf"), -512.0, 512.0 * 15 - HALF, ALU.mult, ALU.add)
-    ts(W("hsubc"), W("pmf"), -512.0, 512.0 * 15, ALU.mult, ALU.add)
-    ts(W("uo", 8, 16), W("uo", 0, 8), 96, None, ALU.bitwise_and)
-    cp(W("uof", 0, 8), W("uo", 8, 16))
-    ts(W("uof", 8, 16), W("uo", 8, 16), 16, None, ALU.add)
-    ts(W("wa"), W("ia"), W("pmf"), None, ALU.add)
-    ts(W("oda"), W("wa"), float(C), W("odd"), ALU.add, ALU.mult)
-    ts(W("mk0"), W("it1"), 15, None, ALU.bitwise_and)
-    ts(W("mk"), W("mk0"), 0.0, None, ALU.is_equal)
-    cp(wl(MY), W("lists", MY, MY + NG))
+    def ahead_wrap(r):
+        wrap(W("rw"), tn)
+        shift("tn%d" % r, tn, tn, EVEN, -1)
+        shift("ll%d" % r, W("ll"), W("rw"), EVEN, 0)
+
     quant("u", W("ut"))
-    uoff = W("uof")
-    qs, qd = W("qu", ind=uoff), W("qu2")
+    cp(wl(TW), W("lists", TW, TW + NG))
+    act(nrow, W("ioc", ind=wl(TW)))
+    qs, qd = W("qu", ind=W("uof")), W("qu2")
     op("v", lambda e: e.tensor_copy(ap(qd, dt.uint32), ap(qs, dt.uint32)), [qs], [qd])
-    ts(W("cb", 0, C), W("mk"), -4.0, 4.0, ALU.mult, ALU.add)
-    gcopy(W("cb", C, 2 * C), W("cb", 0, C))
-    ts(W("ch"), W("mk"), -16896.0, 512.0, ALU.mult, ALU.add)
-    ts(W("cq"), W("mk", 0, 16), -0.25, 0.25, ALU.mult, ALU.add)
-    scan(W("iv4b"), W("cq"), W("mk", 0, 16), ALU.mult, ALU.add)
-    cp(W("inv4"), W("iv4b", 15, 16))
-    ts(W("hsubl"), W("ev"), -float(C), W("hsub"), ALU.mult, ALU.add)
-
-    def hold(row):
-        scan(W("hs"), W("ch"), row, ALU.add, ALU.max)
-        return W("hs", 15, C, 16)
-
-    def masked(out, row):
-        tt(W("wm_"), row, W("mk"), ALU.mult)
-        scan(W("ws_"), W("cb", 0, C), W("wm_"), ALU.mult, ALU.add)
-        ts(out, W("ws_", 15, C, 16), W("inv4"), float(HALF), ALU.mult, ALU.add)
-
-    def ahead_n2():
-        act(W("tn", 0, C), W("tx", ind=wl(NY)))
-        act(W("tn", C, 2 * C), W("tn", 0, C, ind=wl(PY)))
-
-    def ahead_m(r):
-        if r == 0:
-            act(W("rmp"), W("tm", 0, C, ind=wl(PX)))
-        act(W("rl"), W("tm", ind=wl(MX)))
-        if r > 0:
-            act(W("rmp"), W("tm", 0, C, ind=W("wps")))
-            op("y", lambda e: e.dma_start(T.rmw[:], T.rmp[0:128:16, :]), [W("rmp")], [W("rmw")], "drw%d" % r, 16)
-
-    def ahead_w(r):
-        ts(W("lm"), wl(MY), float(HALF), None, ALU.subtract)
-        if r == 0:
-            ts(W("lv"), hold(W("rmp")), W("hsubc"), None, ALU.subtract)
-            tt(W("ld"), W("lv"), W("lm"), ALU.subtract)
-        ts(W("ll"), hold(W("rl")), W("hsubl"), None, ALU.subtract)
-
-    cp(wl(PX), W("lists", PX, PX + NG))
-    act(W("tm", 0, C), W("ioc", ind=wl(MY)))
-    act(W("su2"), W("su", ind=uoff))
-    ts(W("e1"), W("lists", MX, MX + NG), W("ev"), None, ALU.mult)
-    tt(W("e2"), W("e1"), W("oda"), ALU.add)
-    cp(wl(MX), W("e2"))
-    ahead_m(0)
+    cp(wl(OF), W("lists", OF, OF + NG))
+    act(W("su2"), W("su", ind=W("uof")))
+    ahead()
     quant("t0", W("x0", 0, 4 * HALF), 0, HALF)
     quant("t0", W("x0", 4 * HALF, 4 * C), HALF, C)
-    cp(W("wl", 4 * NG, 6 * NG), W("lists", 4 * NG, 6 * NG))
-    cp(W("nyw", 0, C), W("ioc", ind=wl(NY)))
-    cp(wl(PY), W("lists", PY, PY + NG))
-    cp(W("tx"), W("ioc", ind=wl(NX)))
-    for b in range(4):
-        quant("e", W("et", 3 - b, 515 - b), 128 * b, 128 * b + 128)
-    ahead_w(0)
+    cp(wl(PR), W("lists", PR, PR + NG))
+    tt(W("e1"), W("lists", PR, PR + NG), W("wa"), ALU.subtract)
+    tt(W("e2"), W("lists", PR, PR + NG), W("wa"), ALU.add)
+    ts(W("dlt"), W("e1"), 0.5, W("kin2"), ALU.mult, ALU.mult)
+    ts(W("mid"), W("e2"), 0.5, None, ALU.mult)
+    cp(W("wl", NW, NW + 2 * NG), W("lists", NW, NW + 2 * NG))
 
     for r, step in enumerate(STEPS):
         last = r == ROUNDS - 1
-        t = "t%d" % r
+        t, z, hh, k = ["%s%d" % (n, r) for n in ("t", "z", "hh", "k")]
         partner = T.cores[rank ^ step]
         mm(bank("psb", 0, HALF), "u2", 0, t, 0, HALF)
         mm(bank("psb", 1, HALF), "u2", 0, t, HALF, C)
-        mm(bank("psb", 2, C), "u2", 128, t, 0, C)
-        act(W("by", 0, HALF), bank("psb", 0, HALF), AF.Sign, bias=-2.0 ** -100)
-        act(W("by", HALF, C), bank("psb", 1, HALF), AF.Sign, bias=-2.0 ** -100)
+        act(W("sg", 0, HALF), bank("psb", 0, HALF), AF.Sign, bias=-2.0 ** -100)
+        act(W("sg", HALF, C), bank("psb", 1, HALF), AF.Sign, bias=-2.0 ** -100)
+        act(W("sg", C, 2 * C), W("sg", 0, C, ind=wl(PR)))
+        ahead_wrap(r)
+        tt(W("e1"), hold(W("sg", 0, C)), W("dlt"), ALU.mult)
         if r == 0:
-            act(W("nyw", C, 2 * C), W("nyw", 0, C, ind=wl(PY)))
-            ahead_n2()
-        act(W("eb", C, 2 * C), bank("psb", 2, C), AF.Sign, bias=-2.0 ** -100)
-        act(W("eb", 2 * C, 3 * C), W("eb", C, 2 * C, ind=wl(PX)))
-        cp(W("by2"), W("by"))
-        tt(W("eb", 0, C), W("by", ind=wl(PY)), W("by2"), ALU.mult)
-        scan(W("scn", 0, C), W("cb", 0, C), W("eb", 0, C), ALU.mult, ALU.add)
-        ts(W("e1"), W("scn", 15, C, 16), 0.0, float(C), ALU.is_gt, ALU.mult)
-        tt(W("e2"), W("e1"), W("wa"), ALU.add)
-        cp(W("offy"), W("e2"))
+            cp(W("nw"), W("ioc", ind=wl(NW)))
+            for b in range(4):
+                quant("e", W("et", 3 - b, 515 - b), 128 * b, 128 * b + 128)
         for b in range(4):
             mm(bank("psa", b, C), "e", 128 * b, t, 0, C)
-        act(W("nti", C, 2 * C), W("nyw", ind=W("offy")))
-        act(W("q1"), W("tn", ind=W("offy")))
-        for k in range(0, 8, 2):
-            dma("na%d" % r, W("nas", **group(k)), W("nti", C, 2 * C, **group(k + 1)))
-        scan(W("scn", C, 3 * C), W("cb"), W("eb", C, 3 * C), ALU.mult, ALU.add)
-        tt(W("e1"), W("scn", C + 15, 2 * C, 16), W("scn", 2 * C + 15, 3 * C, 16), ALU.mult)
-        ts(W("e2"), W("e1"), 0.0, None, ALU.is_gt)
-        if r > 0:
-            tt(W("ld"), W("rmw"), W("lm"), ALU.subtract)
-        tt(W("e3"), W("e2"), W("ld"), ALU.mult)
-        tt(W("e4"), W("e3"), W("lm"), ALU.add)
-        ts(W("offl"), W("e4"), float(HALF), None, ALU.add)
-        act(W("uu"), W("q1", ind=W("offl")))
-        masked(W("offp"), W("nti", ind=W("ll")))
-        act(plane("fp", 0), bank("psa", 0, C))
-        gcopy(plane("fd", 0), plane("fp", 0))
-        masked(W("offw"), W("uu", ind=W("offp")))
-        for b in range(1, 4):
+        for b in (0, 1):
             act(plane("fp", b), bank("psa", b, C))
-        gcopy(plane("fd", 1), plane("fp", 1))
-        if last:
-            act(W("nlf"), W("nas", ind=W("offw")), AF.Identity, bias=float(HALF))
+        tt(W("e2"), hold(W("sg", C, 2 * C)), W("e1"), ALU.mult)
+        tt(W("e3"), W("e2"), W("mid"), ALU.add)
+        cp(W("ta"), W("e3"))
+        shift("sw%d" % r, W("tb"), W("ta"), EVEN, -1)
+        shift("sw%d" % r, W("tb"), W("ta"), ODD, 1)
+        act(W("nti"), W("nw", ind=W("ta")))
+        shift("na%d" % r, W("nas"), W("nti"), EVEN, 2)
+        cp(W("qb", 0, C), tn[:6] + (W("ta"),))
+        act(W("p4"), W("nti", ind=W("ll")))
+        cp(W("q2"), W("qb", ind=wl(MQ)))
+        act(W("uu"), W("q2", ind=W("tb")))
+        wrap(W("wp"), W("p4"))
+        move("v", W("wr", HALF, C), W("uu", ind=W("wp", 12, 24)))
+        move("s", W("wr", 0, HALF), W("uu", ind=W("wp", 0, 12)))
+        act(plane("fp", 2), bank("psa", 2, C))
+        wrap(W("ww"), W("wr"))
+        move("v", W("nb", C, C + HALF), W("nas", ind=W("ww", 12, 24)))
+        move("s", W("nb", HALF, C), W("nas", ind=W("ww", 0, 12)))
+        act(plane("fp", 3), bank("psa", 3, C))
+        lo, hi = W("wn", 12, 24), W("wn", 24, 36)
+        if SPLIT:
+            wrap(hi, W("nb", C, C + HALF))
+            act(W("nb", 0, HALF), nrow[:6] + (hi,))
+            for b in range(4):
+                act(plane("an", b, HALF, HALF), plane("fp", b, ind=hi))
+            wrap(W("wn", 0, 24), W("nb", 0, C))
+            for b in range(4):
+                tt(W("zt", 4 * HALF + b, 4 * C, 4), plane("fp", b, ind=W("wn", 0, 12)), plane("an", b, HALF, HALF), ALU.add)
+            act(W("nb", HALF + C, 2 * C), nrow[:6] + (lo,))
+            for b in range(2):
+                act(plane("an", b, 0, HALF), plane("fp", b, ind=lo))
+            quant(z, W("zt", 4 * HALF, 4 * C), HALF, C)
+            wrap(W("wn", 36, 48), W("nb", HALF + C, 2 * C))
         else:
-            act(W("tx"), W("nas", ind=W("offw")))
-        masked(W("wn"), W("nas", ind=W("offw")))
+            wrap(nw_, nrow)
+            move("v", W("nb", 2 * C, 2 * C + HALF), nrow[:6] + (hi,))
+            move("s", W("nb", HALF + C, 2 * C), nrow[:6] + (lo,))
+            for b in range(4):
+                act(plane("an", b), plane("fp", b, ind=nw_))
+            wrap(W("wn", 36, 60), W("nb", HALF + C, HALF + 2 * C))
+            for b in range(4):
+                tt(W("zt", b, 4 * C, 4), plane("fp", b, ind=W("wn", 36, 60)), plane("an", b), ALU.add)
+            quant(z, W("zt", 4 * HALF, 4 * C), HALF, C)
+            quant(z, W("zt", 0, 4 * HALF), 0, HALF)
         if not last:
-            for o in range(1, 8, 2):
-                for to in (o, o + 1):
-                    dma("sn%d" % r, W("nyw", 0, C, **group(to)), W("tx", **group(o - 1)))
-                    dma("sn%d" % r, W("wl", NY, NY + NG, **group(to)), W("wn", **group(o - 1)))
-            for o in range(1, 8, 2):
-                dma("sx%d" % r, W("tx", **group(o + 1)), W("tx", **group(o)))
-        hi, lo = W("wn", 12, 24), W("wn", 0, 12)
-        for b in (3, 2):
-            act(plane("kp", b), plane("fp", b, ind=W("wn")))
-        for b in (0, 1):
-            tt(plane("yp", b), plane("fp", b, ind=W("wn")), plane("fd", b), ALU.add)
-        for b in (3, 2):
-            tt(plane("yp", b), bank("psa", b, C), plane("kp", b), ALU.add)
-        for b in (0, 1, 2):
-            act(W("zh", b, 4 * HALF, 4), plane("yp", b, ind=hi), scale=0.5)
-        ts(W("zh", 3, 4 * HALF, 4), plane("yp", 3, ind=hi), 0.5, None, ALU.mult)
-        zh, zl, hh, hl, ld = ["%s%d" % (n, r) for n in ("zh", "zl", "hh", "hl", "ld")]
-        quant(zh, W("zh"))
-        for b in (0, 1):
-            act(W("zl", b, 4 * HALF, 4), plane("yp", b, ind=lo), scale=0.5)
-        ts(W("zl", 2, 4 * HALF, 4), plane("yp", 2, ind=lo), 0.5, None, ALU.mult)
+            shift("n%d" % r, wl(OF), nw_, ODD, -1)
+            shift("n%d" % r, W("nw"), nrow, EVEN, -2)
         for b in range(4):
-            mm(bank("psb", b, HALF), "w", 128 * b, zh, 0, HALF)
+            mm(bank("psb", b, HALF), "w", 128 * b, z, HALF, C)
         for b in range(4):
-            if b % 2 == 0:
-                ts(W("hh", b, 4 * HALF, 4), bank("psb", b, HALF), 0.03125, None, ALU.mult)
-            else:
-                act(W("hh", b, 4 * HALF, 4), bank("psb", b, HALF), scale=0.03125)
+            move("vs"[b % 2], W("hh", b, 4 * HALF, 4), bank("psb", b, HALF), 0.03125)
         quant(hh, W("hh"))
-        act(W("zl", 3, 4 * HALF, 4), plane("yp", 3, ind=lo), scale=0.5)
-        quant(zl, W("zl"))
-        for b in range(4):
-            mm(bank("psa", b, HALF), "w", 128 * b, zl, 0, HALF)
         rid, pid = topo.addr(partner)[:2]
         mask = topo.mask(core, partner)
         arr = "arr%d" % r
         depend("g", [W("q" + hh), W("s" + hh)], [])
-        g.remote_dma(T["q" + ld][:, 0:HALF].bitcast(dt.uint8), T["q" + hh][:, 0:HALF].bitcast(dt.uint8), T.sem[arr], T.sem.snd, pid, rid, mask)
-        g.remote_dma(T["s" + ld][:, 0:HALF], T["s" + hh][:, 0:HALF], T.sem[arr], T.sem.snd, pid, rid, mask)
+        g.remote_dma(T["q" + k][:, HALF:C].bitcast(dt.uint8), T["q" + hh][:, 0:HALF].bitcast(dt.uint8), T.sem[arr], T.sem.snd, pid, rid, mask)
+        g.remote_dma(T["s" + k][:, HALF:C], T["s" + hh][:, 0:HALF], T.sem[arr], T.sem.snd, pid, rid, mask)
         count["snd"] = count.get("snd", 0) + 2 * len(topo.engines(core, partner))
         count[arr] = 2 * len(topo.engines(partner, core))
-        for nm in ("q" + ld, "s" + ld):
-            acc.setdefault(nm, []).append((W(nm), True, "far", arr, count[arr]))
+        for nm in ("q" + k, "s" + k):
+            acc.setdefault(nm, []).append((W(nm, HALF, C), True, "far", arr, count[arr]))
+        if SPLIT:
+            for b in (2, 3):
+                act(plane("an", b, 0, HALF), plane("fp", b, ind=lo))
+            for b in range(4):
+                tt(W("zt", b, 4 * HALF, 4), plane("fp", b, ind=W("wn", 36, 48)), plane("an", b, 0, HALF), ALU.add)
+            quant(z, W("zt", 0, 4 * HALF), 0, HALF)
+        for b in range(4):
+            mm(bank("psa", b, HALF), "w", 128 * b, z, 0, HALF)
         for b in range(4):
             act(W("hl", b, 4 * HALF, 4), bank("psa", b, HALF), scale=0.03125)
-        if not last:
-            ahead_n2()
-        sc = W("rm", ind=W("wn"))
+        sc = W("rm", ind=nw_)
         op("v", lambda e: e.tensor_copy(ap(sc), ap(W("ioc"))), [W("ioc")], [sc])
-        quant(hl, W("hl"))
-        ts(W("wm"), hold(W("rm")), W("hsub"), None, ALU.subtract)
-        if r == 0:
-            cp(W("ptf"), W("pt"))
-            op("v", lambda e: e.transpose(ap(W("ptt")), ap(W("ptf"))), [W("ptf")], [W("ptt")])
-            cp(W("wps"), W("ptt", 0, NG))
-            quant("v", W("vt"))
+        quant(k, W("hl"), 0, HALF)
+        wrap(W("wm"), W("rm"))
         if not last:
-            cp(W("nyw", C, 2 * C), W("nyw", 0, C, ind=wl(PY)))
-        for b in range(4):
-            mm(bank("psb", b, HALF), "e", 128 * b, hl, 0, HALF)
-        for b in range(4):
-            if b % 2 == 0:
-                cp(plane("kp", b, 0, HALF), bank("psb", b, HALF))
-            else:
-                act(plane("kp", b, 0, HALF), bank("psb", b, HALF))
-        if not last:
-            for o in range(1, 8, 2):
-                for to in (o, o + 1):
-                    dma("sm%d" % r, W("tm", 0, C, **group(to)), W("rm", **group(o - 1)))
-            for o in range(1, 8, 2):
-                dma("sk%d" % r, W("wl", MX, MX + NG, **group(o + 1)), W("wm", **group(o)))
-            for o in range(1, 8, 2):
-                for to in (o, o + 1):
-                    dma("sy%d" % r, W("wl", MY, MY + NG, **group(to)), W("wm", **group(o - 1)))
+            shift("m%d" % r, nrow, W("rm"), EVEN, -2)
+            shift("m%d" % r, W("nw"), W("rm"), ODD, -1)
+            shift("mw%d" % r, wl(OF), W("wm"), EVEN, -1)
+            shift("mw%d" % r, wl(MQ), W("wm"), EVEN, -2)
         else:
+            act(W("nlf"), nrow, AF.Identity, bias=float(HALF))
             op("y", lambda e: e.dma_start(T.nl[:], T.nlf[0:128:16, :]), [W("nlf")], [], "do", 16)
-        for b in (3, 0, 1, 2):
-            mm(bank("psa", b, HALF), "e", 128 * b, ld, 0, HALF)
-        for b in (3, 2):
-            mm(bank("psb", b, C), "e", 128 * b, t, 0, C)
-        act(plane("kp", 3, HALF, HALF), bank("psa", 3, HALF))
-        cp(plane("kp", 0, HALF, HALF), bank("psa", 0, HALF))
-        act(plane("yp", 3), plane("kp", 3, ind=W("wm")))
-        for b in (1, 2):
-            act(plane("kp", b, HALF, HALF), bank("psa", b, HALF))
-        act(plane("yp", 2), plane("kp", 2, ind=W("wm")))
+        if r == 0:
+            quant("v", W("vt"))
+        for b in range(4):
+            mm(bank("psb", b, HALF), "e", 128 * b, k, 0, HALF)
+        for b in range(4):
+            tt(plane("xn", b, 0, HALF), bank("psb", b, HALF), plane("an", b, 0, HALF), ALU.add)
+        for b in range(4):
+            mm(bank("psa", b, HALF), "e", 128 * b, k, HALF, C)
+        for b in range(4):
+            tt(plane("xn", b, HALF, HALF), bank("psa", b, HALF), plane("an", b, HALF, HALF), ALU.add)
         for b in (0, 1):
-            tt(W("xt", b, 4 * C, 4), plane("kp", b, ind=W("wm")), plane("fp", b), ALU.add)
-        for b in (3, 2):
-            tt(W("xt", b, 4 * C, 4), bank("psb", b, C), plane("yp", b), ALU.add)
+            move("s", W("xt", b, 4 * C, 4), plane("xn", b, ind=W("wm")), 2.0)
+        move("v", W("xt", 2, 4 * C, 4), plane("xn", 2, ind=W("wm")), 2.0)
+        move("s", W("xt", 3, 4 * HALF, 4), plane("xn", 3, ind=W("wm", 0, 12)), 2.0)
+        move("v", W("xt", 4 * HALF + 3, 4 * C, 4), plane("xn", 3, ind=W("wm", 12, 24)), 2.0)
+        if not last:
+            ahead()
         quant("t%d" % (r + 1), W("xt", 0, 4 * HALF), 0, HALF)
         quant("t%d" % (r + 1), W("xt", 4 * HALF, 4 * C), HALF, C)
-        if not last:
-            ahead_m(r + 1)
-            ahead_w(r + 1)
 
     f = "t%d" % ROUNDS
     mm(bank("psb", 0, HALF), "v", 0, f, 0, HALF)
     mm(bank("psb", 1, HALF), "v", 0, f, HALF, C)
     op("s", lambda e: e.dma_start(T.oc[:], T["q" + f][:, 0:C].bitcast(dt.uint8)), [W("q" + f)], [], "do", 16)
-    for k in range(4):
-        op("y", lambda e: e.dma_start(T.osc[4 * k:4 * k + 4, :], T["s" + f][32 * k:32 * k + 4, 0:C]), [W("s" + f)], [], "do", 16)
+    for q in range(4):
+        op("y", lambda e: e.dma_start(T.osc[4 * q:4 * q + 4, :], T["s" + f][32 * q:32 * q + 4, 0:C]), [W("s" + f)], [], "do", 16)
     cp(W("yo", 0, HALF), bank("psb", 0, HALF))
     act(W("yo", HALF, C), bank("psb", 1, HALF))
     dma("o", T.y[:, 0:HALF], W("yo", 0, HALF))

@@ -4,9 +4,9 @@ C, HALF, NG = 384, 192, 24
 ROUNDS = 3
 STEPS = [1, 2, 3]
 BIG = 2.0 ** 40
+CUT = 128
 ALU = AluOpType
 AF = ActivationFunctionType
-SPLIT = True
 
 SCRATCH = {}
 
@@ -21,15 +21,15 @@ def _mx(name, cols):
 
 
 for _n, _c in (("x0", 4 * C), ("xt", 4 * C), ("ut", 512), ("vt", 512), ("half", 515), ("et", 515), ("zt", 4 * C), ("hh", 4 * HALF), ("hl", 4 * HALF),
-               ("fp", 4 * C), ("an", 4 * C), ("xn", 4 * C), ("ioc", C), ("hk", C), ("hk16", 16), ("sg", 2 * C), ("scn", 4 * C),
-               ("nw", C), ("nti", C), ("qb", 2 * C), ("q2", C), ("p4", C), ("uu", C), ("wr", C), ("nas", C), ("nb", 2 * C + HALF), ("rm", C)):
+               ("fp", 4 * C), ("an", 4 * C), ("xn", 4 * C), ("hk", C), ("hk16", 16), ("sg", 2 * C), ("scn", 6 * C), ("ids", 2 * C), ("tm", C), ("tx", C),
+               ("rl", C), ("nw", C), ("nti", C), ("qb", 2 * C), ("q2", C), ("p4", C), ("uu", C), ("wr", C), ("nas", C), ("nb", 2 * C), ("rm", C), ("m1", C)):
     _sb(_n, _c, "bfloat16")
-for _n, _c in (("ia", NG), ("wa", NG), ("j16", 16), ("ja", 16), ("jb", 16), ("pmf", 1), ("kinv", 1), ("kin2", 1), ("mid", NG), ("dlt", NG),
+for _n, _c in (("ia", NG), ("wa", NG), ("j16", 16), ("ja", 16), ("jb", 16), ("jc", 16), ("pmf", 1), ("kinv", 1), ("kin2", 1), ("mid", NG), ("dlt", NG),
                ("e1", NG), ("e2", NG), ("e3", NG), ("nlf", C), ("yo", C)):
     _sb(_n, _c, "float32")
-for _n, _c in (("ip", 1), ("pm", 1), ("uo", 16), ("lists", 5 * NG)):
+for _n, _c in (("ip", 1), ("pm", 1), ("uo", 16), ("lists", 7 * NG)):
     _sb(_n, _c, "int32")
-for _n, _c in (("uof", 8), ("rep", NG), ("wl", 5 * NG), ("ta", NG), ("tb", NG), ("ll", NG), ("rw", NG), ("wp", NG), ("ww", NG), ("wn", 2 * NG + 12), ("wm", NG)):
+for _n, _c in (("uof", 8), ("rep", NG), ("wl", 6 * NG), ("ta", NG), ("tb", NG), ("ll", NG), ("wp", NG), ("ww", NG), ("wn", 2 * NG), ("wm", NG), ("tc", NG)):
     _sb(_n, _c, "uint16")
 _mx("u", 128)
 _mx("u2", 128)
@@ -45,10 +45,10 @@ for _r in range(ROUNDS):
 SCRATCH["psa"] = ("psum", [128, 2048], "float32")
 SCRATCH["psb"] = ("psum", [128, 2048], "float32")
 
-DMA_GROUPS = ["x", "u", "v", "w", "la", "lb", "lc", "ld", "o"] + ["%s%d" % (n, r) for r in range(ROUNDS) for n in ("sw", "na", "n", "m", "mw", "ll", "tn")]
+DMA_GROUPS = ["x", "xh", "u", "v", "w", "la", "lb", "ld", "lm", "o"] + ["%s%d" % (n, r) for r in range(ROUNDS) for n in ("sw", "na", "n", "m", "mw", "tc", "id")]
 SEMAPHORES = ["cv", "cs", "ct", "cg", "snd"] + ["d" + n for n in DMA_GROUPS] + ["arr%d" % r for r in range(ROUNDS)]
 
-PR, TW, OF, NW, MQ = [NG * k for k in range(5)]
+TX, NY, PR, NW, MQ, MO = [NG * k for k in range(6)]
 EVEN, ODD = range(0, 8, 2), range(1, 8, 2)
 
 
@@ -92,9 +92,7 @@ def rank_program(g, core, T, topo):
             for (rv, rw, rq, sem, val) in acc.get(v[0], []):
                 if not (isw or rw) or not meets(v, rv) or phased(v, rv):
                     continue
-                if not rw and rq == q and q == "t":
-                    continue
-                if rw and isw and rq == q and q == "t":
+                if isw and rq == q and q == "t":
                     continue
                 need[sem] = max(need.get(sem, 0), count[sem] if sem[0] == "d" else val)
         k = known[q]
@@ -178,95 +176,101 @@ def rank_program(g, core, T, topo):
     def bank(n, k, w):
         return W(n, 512 * k, 512 * k + w)
 
-    def wl(k):
-        return W("wl", k, k + NG)
+    def wl(k, a=0, b=NG):
+        return W("wl", k + a, k + b)
+
+    def raw(k, n=1):
+        return W("lists", k, k + n * NG)
 
     def plane(n, b, a=0, w=C, ind=None):
         return W(n, b * C + a, b * C + a + w, ind=ind)
 
+    def by(v, ind):
+        return v[:6] + (ind,)
+
     def part(v, k):
         return v[:4] + (16 * (k % 8), 16 * (k % 8) + 16, None)
 
-    def shift(grp, out, in_, to, by):
+    def shift(grp, out, in_, to, by_, q="y"):
         for k in to:
-            dma(grp, part(out, k), part(in_, k + by))
+            p = 16 * ((k + by_) % 8)
+            dma(grp, part(out, k), part(in_, k + by_) if isinstance(in_, tuple) else in_[p:p + 16, :], q=q)
+
+    def halves(out, window, offsets):
+        for q, a in (("v", 1), ("s", 0)):
+            move(q, W(out[0], out[1] + a * HALF, out[1] + (a + 1) * HALF), by(window, W(offsets[0], offsets[1] + 12 * a, offsets[1] + 12 * a + 12)))
 
     turn = [0]
 
     def hold(row):
-        n, at = row[2] - row[1], C * (turn[0] % 4)
+        n, at = row[2] - row[1], C * (turn[0] % 6)
         turn[0] += 1
         scan(W("scn", at, at + n), W("hk", 0, n), row, 0.0, ALU.mult, ALU.add)
         return W("scn", at + 15, at + n, 16)
 
+    def places(out, held):
+        ts(out, held, W("kinv"), float(HALF), ALU.mult, ALU.add)
+
     def wrap(out, row):
-        ts(out, hold(row), W("kinv"), float(HALF), ALU.mult, ALU.add)
+        places(out, hold(row))
 
-    dma("x", W("x0"), T.x[:])
     dma("u", W("ut"), T.u[:], q="s")
-    for grp, q, k, odd, even in (("la", "s", TW, (T.nx, 0), (T.iv, -2)), ("lb", "y", OF, (T.nx, -1), (T.iv, -1)),
-                                 ("lb", "y", PR, (T.pr, 0), (T.pr, -2)), ("lc", "s", NW, (T.iv, -1), (T.nx, -2))):
-        for to in range(8):
-            src, by = odd if to % 2 else even
-            frm = 16 * ((to + by) % 8)
-            dma(grp, part(W("lists", k, k + NG), to), src[frm:frm + 16, :], q=q)
+    dma("x", W("x0", 0, 4 * HALF), T.x[:, 0:4 * HALF])
+    dma("xh", W("x0", 4 * HALF, 4 * C), T.x[:, 4 * HALF:4 * C])
+    for grp, q, k, odd, even in (("la", "s", TX, (T.nx, 0), (T.nx, -1)), ("la", "y", NY, (T.nx, -1), (T.nx, -2)),
+                                 ("lb", "s", PR, (T.pr, 0), (T.pr, -2)), ("lb", "y", NW, (T.iv, -1), (T.nx, -2))):
+        shift(grp, raw(k), odd[0], ODD, odd[1], q)
+        shift(grp, raw(k), even[0], EVEN, even[1], q)
 
+    ioc, nrow, nw_, tn = W("ids", 0, C), W("nb", HALF, HALF + C), W("wn", 12, 36), W("qb", C, 2 * C)
     iota(W("ip"), [[1, 1]], 0, 1)
-    iota(W("j16"), [[1, 16]], 0, 0)
     iota(W("ia"), [[16, NG]], 0, 0)
+    iota(W("j16"), [[1, 16]], 0, 0)
     iota(W("uo", 0, 8), [[32, 4], [-80, 2]], 96, 0)
     op("v", lambda e: e.memset(ap(W("half")), 0.5), [], [W("half")])
     op("g", lambda e: e.affine_select(ap(W("et")), ap(W("half")), [[-1, 515]], ALU.is_equal, 0.0, 3, 4), [W("half")], [W("et")])
     ts(W("pm"), W("ip"), 15, None, ALU.bitwise_and)
-    scan(W("ioc"), W("half", 0, C), W("half", 0, C), -HALF - 1.0, ALU.add, ALU.add)
+    scan(ioc, W("half", 0, C), W("half", 0, C), -HALF - 1.0, ALU.add, ALU.add)
     cp(W("pmf"), W("pm"))
-    ts(W("uo", 8, 16), W("uo", 0, 8), 127, None, ALU.bitwise_and)
+    cp(W("ids", C, 2 * C), ioc)
     ts(W("wa"), W("ia"), W("pmf"), None, ALU.add)
     ts(W("ja"), W("j16"), W("pmf"), None, ALU.subtract)
-    cp(W("uof"), W("uo", 8, 16))
-    ts(W("lists", MQ, MQ + NG), W("wa"), float(C), None, ALU.add)
-    ts(W("jb"), W("ja"), 1.0, BIG, ALU.is_equal, ALU.mult)
-    ts(W("j16"), W("ja"), 0.0, None, ALU.is_gt)
     ts(W("rep"), W("ia"), 0.0, W("pmf"), ALU.mult, ALU.add)
-    tt(W("hk16"), W("j16"), W("jb"), ALU.max)
+    ts(raw(MQ), W("wa"), float(C), None, ALU.add)
+    cp(raw(MO), W("wa"))
+    ts(W("uo", 8, 16), W("uo", 0, 8), 127, None, ALU.bitwise_and)
+    ts(W("jb"), W("ja"), 1.0, BIG, ALU.is_equal, ALU.mult)
+    ts(W("jc"), W("ja"), 0.0, None, ALU.is_gt)
     ts(W("kinv"), W("pmf"), 15.0, 1.0 / BIG, ALU.is_equal, ALU.max)
+    cp(W("uof"), W("uo", 8, 16))
+    tt(W("hk16"), W("jc"), W("jb"), ALU.max)
     ts(W("kin2"), W("pmf"), 15.0, 1.0 / BIG / BIG, ALU.is_equal, ALU.max)
-    cp(W("ll"), W("wa"))
-    for to in EVEN:
-        frm = 16 * ((to - 2) % 8)
-        dma("ld", part(W("lists", MQ, MQ + NG), to), T.iv[frm:frm + 16, :])
+    shift("ld", raw(MO), T.iv, EVEN, -1)
+    dma("lm", raw(6 * NG), T.iv[:])
+    shift("ld", raw(MQ), T.iv, EVEN, -2, "s")
     op("y", lambda e: e.dma_start(T.qw[:, 0:512].bitcast(dt.uint8), T.wc[:]), [], [W("qw")], "dw", 16)
     dma("w", W("sw"), T.ws[:])
     dma("v", W("vt"), T.v[:])
     act(W("hk"), W("hk16", ind=W("rep")))
-    cp(W("nas"), W("ioc"))
-
-    nrow, nw_, tn = W("nb", HALF, HALF + C), W("wn", 12, 36), W("qb", C, 2 * C)
-
-    def ahead():
-        act(tn, nrow[:6] + (wl(OF),))
-
-    def ahead_wrap(r):
-        wrap(W("rw"), tn)
-        shift("tn%d" % r, tn, tn, EVEN, -1)
-        shift("ll%d" % r, W("ll"), W("rw"), EVEN, 0)
+    cp(W("nas"), ioc)
 
     quant("u", W("ut"))
-    cp(wl(TW), W("lists", TW, TW + NG))
-    act(nrow, W("ioc", ind=wl(TW)))
     qs, qd = W("qu", ind=W("uof")), W("qu2")
     op("v", lambda e: e.tensor_copy(ap(qd, dt.uint32), ap(qs, dt.uint32)), [qs], [qd])
-    cp(wl(OF), W("lists", OF, OF + NG))
     act(W("su2"), W("su", ind=W("uof")))
-    ahead()
     quant("t0", W("x0", 0, 4 * HALF), 0, HALF)
-    quant("t0", W("x0", 4 * HALF, 4 * C), HALF, C)
-    cp(wl(PR), W("lists", PR, PR + NG))
-    tt(W("e1"), W("lists", PR, PR + NG), W("wa"), ALU.subtract)
-    tt(W("e2"), W("lists", PR, PR + NG), W("wa"), ALU.add)
+    for b in range(4):
+        quant("e", W("et", 3 - b, 515 - b), 128 * b, 128 * b + 128)
+        if b == 1:
+            quant("t0", W("x0", 4 * HALF, 4 * C), HALF, C)
+    cp(wl(TX, 0, 2 * NG), raw(TX, 2))
+    cp(W("tx"), by(ioc, wl(TX)))
+    cp(wl(PR, 0, 2 * NG), raw(PR, 2))
+    cp(wl(MQ, 0, 2 * NG), raw(MQ, 2))
+    tt(W("e1"), raw(PR), W("wa"), ALU.subtract)
+    tt(W("e2"), raw(PR), W("wa"), ALU.add)
     ts(W("dlt"), W("e1"), 0.5, W("kin2"), ALU.mult, ALU.mult)
     ts(W("mid"), W("e2"), 0.5, None, ALU.mult)
-    cp(W("wl", NW, NW + 2 * NG), W("lists", NW, NW + 2 * NG))
 
     for r, step in enumerate(STEPS):
         last = r == ROUNDS - 1
@@ -276,68 +280,75 @@ def rank_program(g, core, T, topo):
         mm(bank("psb", 1, HALF), "u2", 0, t, HALF, C)
         act(W("sg", 0, HALF), bank("psb", 0, HALF), AF.Sign, bias=-2.0 ** -100)
         act(W("sg", HALF, C), bank("psb", 1, HALF), AF.Sign, bias=-2.0 ** -100)
-        act(W("sg", C, 2 * C), W("sg", 0, C, ind=wl(PR)))
-        ahead_wrap(r)
-        tt(W("e1"), hold(W("sg", 0, C)), W("dlt"), ALU.mult)
-        if r == 0:
-            cp(W("nw"), W("ioc", ind=wl(NW)))
-            for b in range(4):
-                quant("e", W("et", 3 - b, 515 - b), 128 * b, 128 * b + 128)
+        if r > 0:
+            wrap(W("ll"), W("rl"))
         for b in range(4):
             mm(bank("psa", b, C), "e", 128 * b, t, 0, C)
-        for b in (0, 1):
+        if r > 0:
+            halves(W("sg", C, 2 * C), W("sg", 0, C), wl(PR))
+        for b in range(2):
             act(plane("fp", b), bank("psa", b, C))
-        tt(W("e2"), hold(W("sg", C, 2 * C)), W("e1"), ALU.mult)
+        if r == 0:
+            act(W("nw"), by(ioc, wl(NW)))
+            cp(W("sg", C, 2 * C), W("sg", 0, C, ind=wl(PR)))
+            act(W("tm"), W("ids", ind=wl(MQ)))
+            act(W("rl"), W("tm", ind=wl(MO)))
+            act(tn, W("tx", ind=wl(NY)))
+        own, other = hold(W("sg", 0, C)), hold(W("sg", C, 2 * C))
+        tt(W("e1"), own, W("dlt"), ALU.mult)
+        tt(W("e2"), other, W("e1"), ALU.mult)
         tt(W("e3"), W("e2"), W("mid"), ALU.add)
         cp(W("ta"), W("e3"))
         shift("sw%d" % r, W("tb"), W("ta"), EVEN, -1)
-        shift("sw%d" % r, W("tb"), W("ta"), ODD, 1)
-        act(W("nti"), W("nw", ind=W("ta")))
+        shift("sw%d" % r, W("tb"), W("ta"), ODD, 1, "s")
+        cp(W("nti"), W("nw", ind=W("ta")))
         shift("na%d" % r, W("nas"), W("nti"), EVEN, 2)
-        cp(W("qb", 0, C), tn[:6] + (W("ta"),))
-        act(W("p4"), W("nti", ind=W("ll")))
-        cp(W("q2"), W("qb", ind=wl(MQ)))
-        act(W("uu"), W("q2", ind=W("tb")))
+        act(W("qb", 0, C), by(tn, W("ta")))
+        if r == 0:
+            wrap(W("ll"), W("rl"))
+        cp(W("p4"), W("nti", ind=W("ll")))
+        act(W("q2"), W("qb", ind=wl(MQ)))
         wrap(W("wp"), W("p4"))
-        move("v", W("wr", HALF, C), W("uu", ind=W("wp", 12, 24)))
-        move("s", W("wr", 0, HALF), W("uu", ind=W("wp", 0, 12)))
+        if r == 0:
+            cp(W("wm"), raw(6 * NG))
+        shift("tc%d" % r, W("tc"), W("ta"), EVEN, 2)
+        shift("tc%d" % r, W("tc"), W("ta"), ODD, 0)
+        shift("tc%d" % r, W("wm"), W("wp"), ODD, 1)
+        halves(W("uu"), W("q2"), W("tb"))
+        halves(W("wr"), W("uu"), W("wp"))
         act(plane("fp", 2), bank("psa", 2, C))
         wrap(W("ww"), W("wr"))
-        move("v", W("nb", C, C + HALF), W("nas", ind=W("ww", 12, 24)))
-        move("s", W("nb", HALF, C), W("nas", ind=W("ww", 0, 12)))
+        shift("id%d" % r, W("wr"), ioc, ODD, 0)
+        halves(nrow, W("nas"), W("ww"))
         act(plane("fp", 3), bank("psa", 3, C))
-        lo, hi = W("wn", 12, 24), W("wn", 24, 36)
-        if SPLIT:
-            wrap(hi, W("nb", C, C + HALF))
-            act(W("nb", 0, HALF), nrow[:6] + (hi,))
-            for b in range(4):
-                act(plane("an", b, HALF, HALF), plane("fp", b, ind=hi))
-            wrap(W("wn", 0, 24), W("nb", 0, C))
-            for b in range(4):
-                tt(W("zt", 4 * HALF + b, 4 * C, 4), plane("fp", b, ind=W("wn", 0, 12)), plane("an", b, HALF, HALF), ALU.add)
-            act(W("nb", HALF + C, 2 * C), nrow[:6] + (lo,))
-            for b in range(2):
-                act(plane("an", b, 0, HALF), plane("fp", b, ind=lo))
-            quant(z, W("zt", 4 * HALF, 4 * C), HALF, C)
-            wrap(W("wn", 36, 48), W("nb", HALF + C, 2 * C))
-        else:
-            wrap(nw_, nrow)
-            move("v", W("nb", 2 * C, 2 * C + HALF), nrow[:6] + (hi,))
-            move("s", W("nb", HALF + C, 2 * C), nrow[:6] + (lo,))
-            for b in range(4):
-                act(plane("an", b), plane("fp", b, ind=nw_))
-            wrap(W("wn", 36, 60), W("nb", HALF + C, HALF + 2 * C))
-            for b in range(4):
-                tt(W("zt", b, 4 * C, 4), plane("fp", b, ind=W("wn", 36, 60)), plane("an", b), ALU.add)
-            quant(z, W("zt", 4 * HALF, 4 * C), HALF, C)
-            quant(z, W("zt", 0, 4 * HALF), 0, HALF)
+        lo, hi, lo2, hi2 = W("wn", 12, 24), W("wn", 24, 36), W("wn", 36, 48), W("wn", 0, 12)
+        wrap(hi, W("nb", C, C + HALF))
+        cp(W("nb", 0, HALF), by(nrow, hi))
+        for b in range(4):
+            act(plane("an", b, HALF, HALF), plane("fp", b, ind=hi))
+        h1, h2 = hold(W("nb", 0, HALF)), hold(W("nb", HALF, C))
+        places(hi2, h1)
+        places(lo, h2)
+        for b in range(4):
+            tt(W("zt", 4 * HALF + b, 4 * C, 4), plane("fp", b, ind=hi2), plane("an", b, HALF, HALF), ALU.add)
+        act(W("nb", HALF + C, 2 * C), by(nrow, lo))
+        for b in range(2):
+            act(plane("an", b, 0, HALF), plane("fp", b, ind=lo))
         if not last:
-            shift("n%d" % r, wl(OF), nw_, ODD, -1)
+            shift("n%d" % r, wl(NY), nw_, ODD, -1)
+            shift("n%d" % r, wl(NY), nw_, EVEN, -2)
+            shift("n%d" % r, W("tx"), nrow, ODD, 0)
+            shift("n%d" % r, W("tx"), nrow, EVEN, -1)
             shift("n%d" % r, W("nw"), nrow, EVEN, -2)
+        h1 = hold(W("nb", HALF + C, 2 * C))
+        quant(z, W("zt", 4 * HALF, 4 * C), HALF, C)
+        places(lo2, h1)
+        act(W("m1"), W("wr", ind=W("tc")))
         for b in range(4):
             mm(bank("psb", b, HALF), "w", 128 * b, z, HALF, C)
+        tt(W("zt", 0, 4 * HALF, 4), plane("fp", 0, ind=lo2), plane("an", 0, 0, HALF), ALU.add)
         for b in range(4):
-            move("vs"[b % 2], W("hh", b, 4 * HALF, 4), bank("psb", b, HALF), 0.03125)
+            move("svsv"[b], W("hh", b, 4 * HALF, 4), bank("psb", b, HALF), 0.03125)
         quant(hh, W("hh"))
         rid, pid = topo.addr(partner)[:2]
         mask = topo.mask(core, partner)
@@ -349,24 +360,24 @@ def rank_program(g, core, T, topo):
         count[arr] = 2 * len(topo.engines(partner, core))
         for nm in ("q" + k, "s" + k):
             acc.setdefault(nm, []).append((W(nm, HALF, C), True, "far", arr, count[arr]))
-        if SPLIT:
-            for b in (2, 3):
-                act(plane("an", b, 0, HALF), plane("fp", b, ind=lo))
-            for b in range(4):
-                tt(W("zt", b, 4 * HALF, 4), plane("fp", b, ind=W("wn", 36, 48)), plane("an", b, 0, HALF), ALU.add)
-            quant(z, W("zt", 0, 4 * HALF), 0, HALF)
+        for b in (2, 3):
+            act(plane("an", b, 0, HALF), plane("fp", b, ind=lo))
+        for b in (1, 2, 3):
+            tt(W("zt", b, 4 * HALF, 4), plane("fp", b, ind=lo2), plane("an", b, 0, HALF), ALU.add)
+        act(W("rm"), W("m1", ind=W("wm")))
+        quant(z, W("zt", 0, 4 * HALF), 0, HALF)
+        wrap(W("wm"), W("rm"))
         for b in range(4):
             mm(bank("psa", b, HALF), "w", 128 * b, z, 0, HALF)
         for b in range(4):
-            act(W("hl", b, 4 * HALF, 4), bank("psa", b, HALF), scale=0.03125)
-        sc = W("rm", ind=nw_)
-        op("v", lambda e: e.tensor_copy(ap(sc), ap(W("ioc"))), [W("ioc")], [sc])
+            move("svsv"[b], W("hl", b, 4 * HALF, 4), bank("psa", b, HALF), 0.03125)
         quant(k, W("hl"), 0, HALF)
-        wrap(W("wm"), W("rm"))
         if not last:
-            shift("m%d" % r, nrow, W("rm"), EVEN, -2)
+            act(tn, W("tx", ind=wl(NY)))
+        if not last:
+            shift("m%d" % r, W("tm"), W("rm"), EVEN, -2)
             shift("m%d" % r, W("nw"), W("rm"), ODD, -1)
-            shift("mw%d" % r, wl(OF), W("wm"), EVEN, -1)
+            shift("mw%d" % r, wl(MO), W("wm"), EVEN, -1)
             shift("mw%d" % r, wl(MQ), W("wm"), EVEN, -2)
         else:
             act(W("nlf"), nrow, AF.Identity, bias=float(HALF))
@@ -384,10 +395,10 @@ def rank_program(g, core, T, topo):
         for b in (0, 1):
             move("s", W("xt", b, 4 * C, 4), plane("xn", b, ind=W("wm")), 2.0)
         move("v", W("xt", 2, 4 * C, 4), plane("xn", 2, ind=W("wm")), 2.0)
-        move("s", W("xt", 3, 4 * HALF, 4), plane("xn", 3, ind=W("wm", 0, 12)), 2.0)
-        move("v", W("xt", 4 * HALF + 3, 4 * C, 4), plane("xn", 3, ind=W("wm", 12, 24)), 2.0)
+        move("s", W("xt", 3, 4 * CUT, 4), plane("xn", 3, ind=W("wm", 0, CUT // 16)), 2.0)
+        move("v", W("xt", 4 * CUT + 3, 4 * C, 4), plane("xn", 3, ind=W("wm", CUT // 16, 24)), 2.0)
         if not last:
-            ahead()
+            act(W("rl"), W("tm", ind=wl(MO)))
         quant("t%d" % (r + 1), W("xt", 0, 4 * HALF), 0, HALF)
         quant("t%d" % (r + 1), W("xt", 4 * HALF, 4 * C), HALF, C)
 

@@ -4,7 +4,8 @@ C, HALF, NG = 384, 192, 24
 ROUNDS = 3
 STEPS = [1, 2, 3]
 BIG = 2.0 ** 40
-CUT = 128
+BANKS = ("psa", "psb")
+PIECES = ((0, 128), (128, 256), (256, C))
 ALU = AluOpType
 AF = ActivationFunctionType
 
@@ -20,16 +21,16 @@ def _mx(name, cols):
     _sb("s" + name, cols, "uint8")
 
 
-for _n, _c in (("x0", 4 * C), ("xt", 4 * C), ("ut", 512), ("vt", 512), ("half", 515), ("et", 515), ("zt", 4 * C), ("hh", 4 * HALF), ("hl", 4 * HALF),
-               ("fp", 4 * C), ("an", 4 * C), ("xn", 4 * C), ("hk", C), ("hk16", 16), ("sg", 2 * C), ("scn", 6 * C), ("ids", 2 * C), ("tm", C), ("tx", C),
-               ("rl", C), ("nw", C), ("nti", C), ("qb", 2 * C), ("q2", C), ("p4", C), ("uu", C), ("wr", C), ("nas", C), ("nb", 2 * C), ("rm", C), ("m1", C)):
+for _n, _c in (("x0", 4 * C), ("xt", 4 * C), ("ut", 512), ("vt", 512), ("half", 515), ("et", 515), ("zt", 4 * C), ("ht", 4 * C),
+               ("fp", 4 * C), ("an", 4 * C), ("xn", 4 * C), ("hk", C), ("hk16", 16), ("sg", 2 * C), ("scn", 6 * C), ("tm", C), ("tx", C), ("rl", C),
+               ("nw", C), ("nti", C), ("qb", 2 * C), ("q2", C), ("p4", C), ("uu", C), ("wr", 2 * C), ("nas", C), ("nb", 2 * C), ("rm", C), ("m1", C)):
     _sb(_n, _c, "bfloat16")
 for _n, _c in (("ia", NG), ("wa", NG), ("j16", 16), ("ja", 16), ("jb", 16), ("jc", 16), ("pmf", 1), ("kinv", 1), ("kin2", 1), ("mid", NG), ("dlt", NG),
-               ("e1", NG), ("e2", NG), ("e3", NG), ("nlf", C), ("yo", C)):
+               ("e1", NG), ("e2", NG), ("e3", NG), ("e4", NG), ("nlf", C), ("yo", C)):
     _sb(_n, _c, "float32")
-for _n, _c in (("ip", 1), ("pm", 1), ("uo", 16), ("lists", 7 * NG)):
+for _n, _c in (("ip", 1), ("pm", 1), ("uo", 16), ("lists", 6 * NG)):
     _sb(_n, _c, "int32")
-for _n, _c in (("uof", 8), ("rep", NG), ("wl", 6 * NG), ("ta", NG), ("tb", NG), ("ll", NG), ("wp", NG), ("ww", NG), ("wn", 2 * NG), ("wm", NG), ("tc", NG)):
+for _n, _c in (("uof", 8), ("rep", NG), ("wl", 8 * NG), ("ta", NG), ("tb", NG), ("tc", NG), ("ll", NG), ("wp", NG), ("ww", NG), ("wn", 2 * NG), ("wm", NG)):
     _sb(_n, _c, "uint16")
 _mx("u", 128)
 _mx("u2", 128)
@@ -40,15 +41,15 @@ for _r in range(ROUNDS + 1):
     _mx("t%d" % _r, C)
 for _r in range(ROUNDS):
     _mx("z%d" % _r, C)
-    _mx("hh%d" % _r, HALF)
+    _mx("o%d" % _r, HALF)
     _mx("k%d" % _r, C)
-SCRATCH["psa"] = ("psum", [128, 2048], "float32")
-SCRATCH["psb"] = ("psum", [128, 2048], "float32")
+for _n in BANKS:
+    SCRATCH[_n] = ("psum", [128, 2048], "float32")
 
-DMA_GROUPS = ["x", "xh", "u", "v", "w", "la", "lb", "ld", "lm", "o"] + ["%s%d" % (n, r) for r in range(ROUNDS) for n in ("sw", "na", "n", "m", "mw", "tc", "id")]
+DMA_GROUPS = ["x", "xh", "u", "v", "w", "la", "lb", "ld", "le", "lf", "o"] + ["%s%d" % (n, r) for r in range(ROUNDS) for n in ("sw", "na", "n", "m", "mw", "tc")]
 SEMAPHORES = ["cv", "cs", "ct", "cg", "snd"] + ["d" + n for n in DMA_GROUPS] + ["arr%d" % r for r in range(ROUNDS)]
 
-TX, NY, PR, NW, MQ, MO = [NG * k for k in range(6)]
+TW, OF, PR, NW, MQ, OWN, NY, MO = [NG * k for k in range(8)]
 EVEN, ODD = range(0, 8, 2), range(1, 8, 2)
 
 
@@ -62,7 +63,7 @@ def rank_program(g, core, T, topo):
         return
 
     queues = {"v": g.vector, "s": g.scalar, "t": g.tensor, "g": g, "y": g.sync}
-    count, known, acc, snaps = {}, {q: {} for q in queues}, {}, {}
+    count, known, acc, snaps, waited = {}, {q: {} for q in queues}, {}, {}, {}
 
     def ap(v, bits=None):
         n, a, b, st, p0, p1, ind = v
@@ -102,6 +103,7 @@ def rank_program(g, core, T, topo):
                 continue
             queues[q].wait_ge(T.sem[sem], val)
             k[sem] = val
+            waited[sem] = max(waited.get(sem, 0), val)
             for s2, v2 in snaps.get((sem, val), {}).items():
                 k[s2] = max(k.get(s2, 0), v2)
 
@@ -150,6 +152,9 @@ def rank_program(g, core, T, topo):
     def act(out, in_, func=AF.Copy, **kw):
         op("s", lambda e: e.activation(ap(out), ap(in_), func, **kw), [in_], [out])
 
+    def gcopy(out, in_):
+        op("g", lambda e: e.affine_select(ap(out), ap(in_), [[0, C]], ALU.is_gt, 0.0, 1, 0), [in_], [out])
+
     def move(q, out, in_, scale=None):
         if q == "s":
             act(out, in_) if scale is None else act(out, in_, scale=scale)
@@ -173,11 +178,11 @@ def rank_program(g, core, T, topo):
         l, ls, r, rs = W("q" + ln, la, la + 128), W("s" + ln, la, la + 128), W("q" + rn, ra, rb), W("s" + rn, ra, rb)
         op("t", lambda e: e.matmul_mx(ap(out), ap(l), ap(ls), ap(r), ap(rs), True, True), [l, ls, r, rs], [out])
 
-    def bank(n, k, w):
-        return W(n, 512 * k, 512 * k + w)
+    def bank(n, k, w, a=0):
+        return W(n, 512 * k + a, 512 * k + a + w)
 
-    def wl(k, a=0, b=NG):
-        return W("wl", k + a, k + b)
+    def wl(k, n=1):
+        return W("wl", k, k + n * NG)
 
     def raw(k, n=1):
         return W("lists", k, k + n * NG)
@@ -196,16 +201,21 @@ def rank_program(g, core, T, topo):
             p = 16 * ((k + by_) % 8)
             dma(grp, part(out, k), part(in_, k + by_) if isinstance(in_, tuple) else in_[p:p + 16, :], q=q)
 
-    def halves(out, window, offsets):
-        for q, a in (("v", 1), ("s", 0)):
-            move(q, W(out[0], out[1] + a * HALF, out[1] + (a + 1) * HALF), by(window, W(offsets[0], offsets[1] + 12 * a, offsets[1] + 12 * a + 12)))
+    def halves(out, window, offsets, cut=HALF):
+        for q, a, b in (("v", cut, out[2] - out[1]), ("s", 0, cut)):
+            move(q, W(out[0], out[1] + a, out[1] + b), by(window, W(offsets[0], offsets[1] + a // 16, offsets[1] + b // 16)))
 
     turn = [0]
 
-    def hold(row):
-        n, at = row[2] - row[1], C * (turn[0] % 6)
+    def slot():
         turn[0] += 1
-        scan(W("scn", at, at + n), W("hk", 0, n), row, 0.0, ALU.mult, ALU.add)
+        return C * (turn[0] % 6)
+
+    def hold(row, pieces=None, at=None):
+        n = row[2] - row[1]
+        at = slot() if at is None else at
+        for a, b in pieces or ((0, n),):
+            scan(W("scn", at + a, at + b), W("hk", a, b), W(row[0], row[1] + a, row[1] + b), 0.0, ALU.mult, ALU.add)
         return W("scn", at + 15, at + n, 16)
 
     def places(out, held):
@@ -214,15 +224,25 @@ def rank_program(g, core, T, topo):
     def wrap(out, row):
         places(out, hold(row))
 
-    dma("u", W("ut"), T.u[:], q="s")
-    dma("x", W("x0", 0, 4 * HALF), T.x[:, 0:4 * HALF])
-    dma("xh", W("x0", 4 * HALF, 4 * C), T.x[:, 4 * HALF:4 * C])
-    for grp, q, k, odd, even in (("la", "s", TX, (T.nx, 0), (T.nx, -1)), ("la", "y", NY, (T.nx, -1), (T.nx, -2)),
-                                 ("lb", "s", PR, (T.pr, 0), (T.pr, -2)), ("lb", "y", NW, (T.iv, -1), (T.nx, -2))):
+    def mask_of(c):
+        m = -1
+        for s in STEPS:
+            m &= topo.mask(c, T.cores[T.rank_of(c) ^ s])
+        return m
+
+    def load(grp, q, k, odd, even):
         shift(grp, raw(k), odd[0], ODD, odd[1], q)
         shift(grp, raw(k), even[0], EVEN, even[1], q)
 
-    ioc, nrow, nw_, tn = W("ids", 0, C), W("nb", HALF, HALF + C), W("wn", 12, 36), W("qb", C, 2 * C)
+    dma("u", W("ut"), T.u[:], q="s")
+    dma("x", W("x0", 0, 4 * HALF), T.x[:, 0:4 * HALF])
+    load("la", "s", TW, (T.nx, 0), (T.iv, -2))
+    load("la", "y", OF, (T.nx, -1), (T.iv, -1))
+    dma("xh", W("x0", 4 * HALF, 4 * C), T.x[:, 4 * HALF:4 * C])
+    load("lb", "s", PR, (T.pr, 0), (T.pr, -2))
+    load("lb", "y", NW, (T.iv, -1), (T.nx, -2))
+
+    wr, ids, nrow, nw_, tn = W("wr", 0, C), W("wr", C, 2 * C), W("nb", HALF, HALF + C), W("wn", 12, 36), W("qb", C, 2 * C)
     iota(W("ip"), [[1, 1]], 0, 1)
     iota(W("ia"), [[16, NG]], 0, 0)
     iota(W("j16"), [[1, 16]], 0, 0)
@@ -230,14 +250,11 @@ def rank_program(g, core, T, topo):
     op("v", lambda e: e.memset(ap(W("half")), 0.5), [], [W("half")])
     op("g", lambda e: e.affine_select(ap(W("et")), ap(W("half")), [[-1, 515]], ALU.is_equal, 0.0, 3, 4), [W("half")], [W("et")])
     ts(W("pm"), W("ip"), 15, None, ALU.bitwise_and)
-    scan(ioc, W("half", 0, C), W("half", 0, C), -HALF - 1.0, ALU.add, ALU.add)
+    scan(ids, W("half", 0, C), W("half", 0, C), -HALF - 1.0, ALU.add, ALU.add)
     cp(W("pmf"), W("pm"))
-    cp(W("ids", C, 2 * C), ioc)
     ts(W("wa"), W("ia"), W("pmf"), None, ALU.add)
     ts(W("ja"), W("j16"), W("pmf"), None, ALU.subtract)
     ts(W("rep"), W("ia"), 0.0, W("pmf"), ALU.mult, ALU.add)
-    ts(raw(MQ), W("wa"), float(C), None, ALU.add)
-    cp(raw(MO), W("wa"))
     ts(W("uo", 8, 16), W("uo", 0, 8), 127, None, ALU.bitwise_and)
     ts(W("jb"), W("ja"), 1.0, BIG, ALU.is_equal, ALU.mult)
     ts(W("jc"), W("ja"), 0.0, None, ALU.is_gt)
@@ -245,85 +262,108 @@ def rank_program(g, core, T, topo):
     cp(W("uof"), W("uo", 8, 16))
     tt(W("hk16"), W("jc"), W("jb"), ALU.max)
     ts(W("kin2"), W("pmf"), 15.0, 1.0 / BIG / BIG, ALU.is_equal, ALU.max)
-    shift("ld", raw(MO), T.iv, EVEN, -1)
-    dma("lm", raw(6 * NG), T.iv[:])
-    shift("ld", raw(MQ), T.iv, EVEN, -2, "s")
+    ts(raw(MQ), W("wa"), float(C), None, ALU.add)
+    shift("ld", raw(MQ), T.iv, EVEN, -2)
+    dma("ld", raw(OWN), T.iv[:])
     op("y", lambda e: e.dma_start(T.qw[:, 0:512].bitcast(dt.uint8), T.wc[:]), [], [W("qw")], "dw", 16)
     dma("w", W("sw"), T.ws[:])
     dma("v", W("vt"), T.v[:])
     act(W("hk"), W("hk16", ind=W("rep")))
-    cp(W("nas"), ioc)
+    for o in (W("nas"), W("tm")):
+        gcopy(o, ids)
 
     quant("u", W("ut"))
     qs, qd = W("qu", ind=W("uof")), W("qu2")
     op("v", lambda e: e.tensor_copy(ap(qd, dt.uint32), ap(qs, dt.uint32)), [qs], [qd])
     act(W("su2"), W("su", ind=W("uof")))
     quant("t0", W("x0", 0, 4 * HALF), 0, HALF)
+    cp(wl(TW, 2), raw(TW, 2))
+    act(W("tx"), by(ids, wl(TW)))
     for b in range(4):
         quant("e", W("et", 3 - b, 515 - b), 128 * b, 128 * b + 128)
         if b == 1:
             quant("t0", W("x0", 4 * HALF, 4 * C), HALF, C)
-    cp(wl(TX, 0, 2 * NG), raw(TX, 2))
-    cp(W("tx"), by(ioc, wl(TX)))
-    cp(wl(PR, 0, 2 * NG), raw(PR, 2))
-    cp(wl(MQ, 0, 2 * NG), raw(MQ, 2))
+    cp(wl(PR, 2), raw(PR, 2))
     tt(W("e1"), raw(PR), W("wa"), ALU.subtract)
     tt(W("e2"), raw(PR), W("wa"), ALU.add)
+    cp(W("ll"), W("wa"))
     ts(W("dlt"), W("e1"), 0.5, W("kin2"), ALU.mult, ALU.mult)
     ts(W("mid"), W("e2"), 0.5, None, ALU.mult)
 
     for r, step in enumerate(STEPS):
         last = r == ROUNDS - 1
-        t, z, hh, k = ["%s%d" % (n, r) for n in ("t", "z", "hh", "k")]
+        t, z, out, k = ["%s%d" % (n, r) for n in ("t", "z", "o", "k")]
         partner = T.cores[rank ^ step]
-        mm(bank("psb", 0, HALF), "u2", 0, t, 0, HALF)
-        mm(bank("psb", 1, HALF), "u2", 0, t, HALF, C)
-        act(W("sg", 0, HALF), bank("psb", 0, HALF), AF.Sign, bias=-2.0 ** -100)
-        act(W("sg", HALF, C), bank("psb", 1, HALF), AF.Sign, bias=-2.0 ** -100)
-        if r > 0:
-            wrap(W("ll"), W("rl"))
+        pieces = PIECES if r else ((0, HALF), (HALF, C))
+        for j, (a, b) in enumerate(pieces):
+            mm(bank("psb", j, b - a), "u2", 0, t, a, b)
+        for j, (a, b) in enumerate(pieces):
+            if r > 0:
+                ts(W("sg", a, b), bank("psb", j, b - a), 0.0, 0.5, ALU.is_gt, ALU.subtract)
+            else:
+                act(W("sg", a, b), bank("psb", j, b - a), AF.Sign, bias=-2.0 ** -100)
+            if r == 0 and j == 0:
+                act(tn, W("tx", ind=wl(OF)))
         for b in range(4):
             mm(bank("psa", b, C), "e", 128 * b, t, 0, C)
         if r > 0:
+            own = hold(W("sg", 0, C), ((0, 256), (256, C)))
             halves(W("sg", C, 2 * C), W("sg", 0, C), wl(PR))
+        else:
+            at = slot()
+            hold(W("sg", 0, C), ((0, HALF),), at)
+            h1 = hold(tn)
+            shift("le", tn, tn, EVEN, -1)
+            halves(W("sg", C, 2 * C), W("sg", 0, C), wl(PR))
+            places(W("wp"), h1)
+            shift("lf", W("ll"), W("wp"), EVEN, 0)
+            own = hold(W("sg", 0, C), ((HALF, C),), at)
+            act(W("nw"), by(ids, wl(NW)))
         for b in range(2):
             act(plane("fp", b), bank("psa", b, C))
+        if r > 0:
+            tt(W("e1"), own, W("dlt"), ALU.mult)
+        other = hold(W("sg", C, 2 * C))
         if r == 0:
-            act(W("nw"), by(ioc, wl(NW)))
-            cp(W("sg", C, 2 * C), W("sg", 0, C, ind=wl(PR)))
-            act(W("tm"), W("ids", ind=wl(MQ)))
-            act(W("rl"), W("tm", ind=wl(MO)))
-            act(tn, W("tx", ind=wl(NY)))
-        own, other = hold(W("sg", 0, C)), hold(W("sg", C, 2 * C))
-        tt(W("e1"), own, W("dlt"), ALU.mult)
+            tt(W("e1"), own, W("dlt"), ALU.mult)
+        else:
+            h1 = hold(W("rl"))
         tt(W("e2"), other, W("e1"), ALU.mult)
+        if r > 0:
+            places(W("ll"), h1)
         tt(W("e3"), W("e2"), W("mid"), ALU.add)
+        shift("sw%d" % r, W("e4"), W("e3"), EVEN, -1)
+        shift("sw%d" % r, W("e4"), W("e3"), ODD[3:], 1)
+        shift("sw%d" % r, W("e4"), W("e3"), ODD[:3], 1, "s")
         cp(W("ta"), W("e3"))
-        shift("sw%d" % r, W("tb"), W("ta"), EVEN, -1)
-        shift("sw%d" % r, W("tb"), W("ta"), ODD, 1, "s")
         cp(W("nti"), W("nw", ind=W("ta")))
+        ts(W("tc"), W("ta"), float(C), None, ALU.add)
         shift("na%d" % r, W("nas"), W("nti"), EVEN, 2)
         act(W("qb", 0, C), by(tn, W("ta")))
         if r == 0:
-            wrap(W("ll"), W("rl"))
+            cp(wl(MQ), raw(MQ))
         cp(W("p4"), W("nti", ind=W("ll")))
         act(W("q2"), W("qb", ind=wl(MQ)))
-        wrap(W("wp"), W("p4"))
+        cp(plane("fp", 2, HALF, HALF), bank("psa", 2, HALF, HALF))
+        cp(W("tb"), W("e4"))
+        h1 = hold(W("p4"))
+        halves(W("uu"), W("q2"), W("tb"), 224)
+        places(W("wp"), h1)
         if r == 0:
-            cp(W("wm"), raw(6 * NG))
+            ts(W("dlt"), W("dlt"), 4.0, None, ALU.mult)
+            cp(W("wm"), raw(OWN))
+            cp(wl(MO), W("wa"))
         shift("tc%d" % r, W("tc"), W("ta"), EVEN, 2)
-        shift("tc%d" % r, W("tc"), W("ta"), ODD, 0)
         shift("tc%d" % r, W("wm"), W("wp"), ODD, 1)
-        halves(W("uu"), W("q2"), W("tb"))
-        halves(W("wr"), W("uu"), W("wp"))
-        act(plane("fp", 2), bank("psa", 2, C))
-        wrap(W("ww"), W("wr"))
-        shift("id%d" % r, W("wr"), ioc, ODD, 0)
-        halves(nrow, W("nas"), W("ww"))
+        halves(wr, W("uu"), W("wp"))
         act(plane("fp", 3), bank("psa", 3, C))
+        act(plane("fp", 2, 0, HALF), bank("psa", 2, HALF))
+        places(W("ww"), hold(wr, ((HALF, C), (0, HALF))))
+        halves(W("nb", C, C + HALF), W("nas"), W("ww", 12, 24), 96)
+        act(W("nb", HALF, C), W("nas", ind=W("ww", 0, 12)))
         lo, hi, lo2, hi2 = W("wn", 12, 24), W("wn", 24, 36), W("wn", 36, 48), W("wn", 0, 12)
         wrap(hi, W("nb", C, C + HALF))
-        cp(W("nb", 0, HALF), by(nrow, hi))
+        halves(W("nb", 0, HALF), nrow, hi, 96)
         for b in range(4):
             act(plane("an", b, HALF, HALF), plane("fp", b, ind=hi))
         h1, h2 = hold(W("nb", 0, HALF)), hold(W("nb", HALF, C))
@@ -337,80 +377,112 @@ def rank_program(g, core, T, topo):
         if not last:
             shift("n%d" % r, wl(NY), nw_, ODD, -1)
             shift("n%d" % r, wl(NY), nw_, EVEN, -2)
-            shift("n%d" % r, W("tx"), nrow, ODD, 0)
-            shift("n%d" % r, W("tx"), nrow, EVEN, -1)
             shift("n%d" % r, W("nw"), nrow, EVEN, -2)
+            gcopy(W("tx"), nrow)
+            shift("n%d" % r, W("tx"), nrow, EVEN, -1)
         h1 = hold(W("nb", HALF + C, 2 * C))
-        quant(z, W("zt", 4 * HALF, 4 * C), HALF, C)
+        quant(out, W("zt", 4 * HALF, 4 * C))
         places(lo2, h1)
-        act(W("m1"), W("wr", ind=W("tc")))
-        for b in range(4):
-            mm(bank("psb", b, HALF), "w", 128 * b, z, HALF, C)
-        tt(W("zt", 0, 4 * HALF, 4), plane("fp", 0, ind=lo2), plane("an", 0, 0, HALF), ALU.add)
-        for b in range(4):
-            move("svsv"[b], W("hh", b, 4 * HALF, 4), bank("psb", b, HALF), 0.03125)
-        quant(hh, W("hh"))
         rid, pid = topo.addr(partner)[:2]
-        mask = topo.mask(core, partner)
         arr = "arr%d" % r
-        depend("g", [W("q" + hh), W("s" + hh)], [])
-        g.remote_dma(T["q" + k][:, HALF:C].bitcast(dt.uint8), T["q" + hh][:, 0:HALF].bitcast(dt.uint8), T.sem[arr], T.sem.snd, pid, rid, mask)
-        g.remote_dma(T["s" + k][:, HALF:C], T["s" + hh][:, 0:HALF], T.sem[arr], T.sem.snd, pid, rid, mask)
-        count["snd"] = count.get("snd", 0) + 2 * len(topo.engines(core, partner))
-        count[arr] = 2 * len(topo.engines(partner, core))
-        for nm in ("q" + k, "s" + k):
+        depend("g", [W("q" + out), W("s" + out)], [])
+        g.remote_dma(T["q" + z][:, HALF:C].bitcast(dt.uint8), T["q" + out][:, 0:HALF].bitcast(dt.uint8), T.sem[arr], T.sem.snd, pid, rid, mask_of(core))
+        g.remote_dma(T["s" + z][:, HALF:C], T["s" + out][:, 0:HALF], T.sem[arr], T.sem.snd, pid, rid, mask_of(core))
+        count["snd"] = count.get("snd", 0) + 2 * bin(mask_of(core)).count("1")
+        count[arr] = 2 * bin(mask_of(partner)).count("1")
+        for nm in ("q" + z, "s" + z):
             acc.setdefault(nm, []).append((W(nm, HALF, C), True, "far", arr, count[arr]))
         for b in (2, 3):
             act(plane("an", b, 0, HALF), plane("fp", b, ind=lo))
-        for b in (1, 2, 3):
+        for b in range(4):
             tt(W("zt", b, 4 * HALF, 4), plane("fp", b, ind=lo2), plane("an", b, 0, HALF), ALU.add)
+        act(W("m1"), W("wr", ind=W("tc")))
         act(W("rm"), W("m1", ind=W("wm")))
         quant(z, W("zt", 0, 4 * HALF), 0, HALF)
-        wrap(W("wm"), W("rm"))
-        for b in range(4):
-            mm(bank("psa", b, HALF), "w", 128 * b, z, 0, HALF)
-        for b in range(4):
-            move("svsv"[b], W("hl", b, 4 * HALF, 4), bank("psa", b, HALF), 0.03125)
-        quant(k, W("hl"), 0, HALF)
-        if not last:
-            act(tn, W("tx", ind=wl(NY)))
-        if not last:
-            shift("m%d" % r, W("tm"), W("rm"), EVEN, -2)
-            shift("m%d" % r, W("nw"), W("rm"), ODD, -1)
-            shift("mw%d" % r, wl(MO), W("wm"), EVEN, -1)
-            shift("mw%d" % r, wl(MQ), W("wm"), EVEN, -2)
-        else:
-            act(W("nlf"), nrow, AF.Identity, bias=float(HALF))
-            op("y", lambda e: e.dma_start(T.nl[:], T.nlf[0:128:16, :]), [W("nlf")], [], "do", 16)
         if r == 0:
             quant("v", W("vt"))
+
+        def product(name, rhs, h):
+            for b in range(4):
+                mm(bank(BANKS[h], b, HALF), name, 128 * b, rhs, HALF * h, HALF * h + HALF)
+
+        def scaled(q, h, b):
+            move(q, W("ht", 4 * HALF * h + b, 4 * HALF * (h + 1), 4), bank(BANKS[h], b, HALF), 0.03125)
+
+        def packed(h):
+            quant(k, W("ht", 4 * HALF * h, 4 * HALF * (h + 1)), HALF * h, HALF * h + HALF)
+
+        def added(h, planes):
+            for b in planes:
+                tt(plane("xn", b, HALF * h, HALF), bank(BANKS[h], b, HALF), plane("an", b, HALF * h, HALF), ALU.add)
+
+        def inverse(held):
+            places(W("wm"), held)
+            if not last:
+                g.sync.wait_ge(T.sem.snd, count["snd"])
+                shift("m%d" % r, W("tm"), W("rm"), EVEN, -2)
+                shift("m%d" % r, wl(MO), W("wm"), EVEN, -1)
+                shift("mw%d" % r, W("nw"), W("rm"), ODD, -1)
+                shift("mw%d" % r, wl(MQ), W("wm"), EVEN, -2)
+
+        def beside():
+            if not last:
+                act(tn, W("tx", ind=wl(NY)))
+            else:
+                act(W("nlf"), nrow, AF.Identity, bias=float(HALF))
+                op("y", lambda e: e.dma_start(T.nl[:], T.nlf[0:128:16, :]), [W("nlf")], [], "do", 16)
+
+        product("w", z, 0)
+        if r > 0:
+            product("w", z, 1)
         for b in range(4):
-            mm(bank("psb", b, HALF), "e", 128 * b, k, 0, HALF)
-        for b in range(4):
-            tt(plane("xn", b, 0, HALF), bank("psb", b, HALF), plane("an", b, 0, HALF), ALU.add)
-        for b in range(4):
-            mm(bank("psa", b, HALF), "e", 128 * b, k, HALF, C)
-        for b in range(4):
-            tt(plane("xn", b, HALF, HALF), bank("psa", b, HALF), plane("an", b, HALF, HALF), ALU.add)
+            scaled("svsv"[b], 0, b)
+        if r == 0:
+            h1 = hold(W("rm"))
+            packed(0)
+            inverse(h1)
+            beside()
+            product("e", k, 0)
+            added(0, range(4))
+            product("w", z, 1)
+            for b in range(4):
+                scaled("svsv"[b], 1, b)
+            packed(1)
+            product("e", k, 1)
+            added(1, range(4))
+        else:
+            scaled("s", 1, 0)
+            h1 = hold(W("rm"))
+            packed(0)
+            inverse(h1)
+            for q, b in (("v", 1), ("s", 2), ("v", 3)):
+                scaled(q, 1, b)
+            product("e", k, 0)
+            packed(1)
+            product("e", k, 1)
+            beside()
+            for h, planes in ((0, (0, 1, 2)), (1, (0, 1)), (0, (3,)), (1, (2, 3))):
+                added(h, planes)
         for b in (0, 1):
             move("s", W("xt", b, 4 * C, 4), plane("xn", b, ind=W("wm")), 2.0)
         move("v", W("xt", 2, 4 * C, 4), plane("xn", 2, ind=W("wm")), 2.0)
-        move("s", W("xt", 3, 4 * CUT, 4), plane("xn", 3, ind=W("wm", 0, CUT // 16)), 2.0)
-        move("v", W("xt", 4 * CUT + 3, 4 * C, 4), plane("xn", 3, ind=W("wm", CUT // 16, 24)), 2.0)
+        cut = 128 if r else 96
+        move("s", W("xt", 3, 4 * cut, 4), plane("xn", 3, ind=W("wm", 0, cut // 16)), 2.0)
+        move("v", W("xt", 4 * cut + 3, 4 * C, 4), plane("xn", 3, ind=W("wm", cut // 16, NG)), 2.0)
         if not last:
             act(W("rl"), W("tm", ind=wl(MO)))
-        quant("t%d" % (r + 1), W("xt", 0, 4 * HALF), 0, HALF)
-        quant("t%d" % (r + 1), W("xt", 4 * HALF, 4 * C), HALF, C)
+        for a, b in PIECES:
+            quant("t%d" % (r + 1), W("xt", 4 * a, 4 * b), a, b)
 
     f = "t%d" % ROUNDS
-    mm(bank("psb", 0, HALF), "v", 0, f, 0, HALF)
-    mm(bank("psb", 1, HALF), "v", 0, f, HALF, C)
+    for j, (a, b) in enumerate(PIECES):
+        mm(bank("psb", j, b - a), "v", 0, f, a, b)
     op("s", lambda e: e.dma_start(T.oc[:], T["q" + f][:, 0:C].bitcast(dt.uint8)), [W("q" + f)], [], "do", 16)
     for q in range(4):
         op("y", lambda e: e.dma_start(T.osc[4 * q:4 * q + 4, :], T["s" + f][32 * q:32 * q + 4, 0:C]), [W("s" + f)], [], "do", 16)
-    cp(W("yo", 0, HALF), bank("psb", 0, HALF))
-    act(W("yo", HALF, C), bank("psb", 1, HALF))
-    dma("o", T.y[:, 0:HALF], W("yo", 0, HALF))
-    dma("o", T.y[:, HALF:C], W("yo", HALF, C), q="s")
-    for sem in sorted(count):
-        g.wait_ge(T.sem[sem], count[sem])
+    for j, (a, b) in enumerate(PIECES):
+        move("vsv"[j], W("yo", a, b), bank("psb", j, b - a))
+    dma("o", T.y[:], W("yo"))
+    for sem in sorted(count, key=lambda m: (m == "do", m)):
+        if waited.get(sem, 0) < count[sem]:
+            g.wait_ge(T.sem[sem], count[sem])

from concourse.mybir import dt, AluOpType, ActivationFunctionType

C, HALF, NG = 384, 192, 24
ROUNDS = 3
STEPS = [1, 2, 3]
BIG = 2.0 ** 40
BANKS = ("psa", "psb")
PIECES = ((0, 128), (128, 256), (256, C))
ALU = AluOpType
AF = ActivationFunctionType

SCRATCH = {}


def _sb(name, cols, dtype):
    SCRATCH[name] = ("sbuf", [128, cols], dtype)


def _mx(name, cols):
    _sb("q" + name, cols, "float8_e4m3fn_x4")
    _sb("s" + name, cols, "uint8")


for _n, _c in (("x0", 4 * C), ("xt", 4 * C), ("ut", 512), ("vt", 512), ("half", 515), ("et", 515), ("zt", 4 * C), ("ht", 4 * C),
               ("fp", 4 * C), ("an", 4 * C), ("xn", 4 * C), ("hk", C), ("hk16", 16), ("sg", 2 * C), ("scn", 6 * C), ("tm", C), ("tx", C), ("rl", C),
               ("nw", C), ("nti", C), ("qb", 2 * C), ("q2", C), ("p4", C), ("uu", C), ("wr", 2 * C), ("nas", C), ("nb", 2 * C), ("rm", C), ("m1", C)):
    _sb(_n, _c, "bfloat16")
for _n, _c in (("ia", NG), ("wa", NG), ("j16", 16), ("ja", 16), ("jb", 16), ("jc", 16), ("pmf", 1), ("kinv", 1), ("kin2", 1), ("mid", NG), ("dlt", NG),
               ("e1", NG), ("e2", NG), ("e3", NG), ("e4", NG), ("nlf", C), ("yo", C)):
    _sb(_n, _c, "float32")
for _n, _c in (("ip", 1), ("pm", 1), ("uo", 16), ("lists", 6 * NG)):
    _sb(_n, _c, "int32")
for _n, _c in (("uof", 8), ("rep", NG), ("wl", 8 * NG), ("ta", NG), ("tb", NG), ("tc", NG), ("ll", NG), ("wp", NG), ("ww", NG), ("wn", 2 * NG), ("wm", NG)):
    _sb(_n, _c, "uint16")
_mx("u", 128)
_mx("u2", 128)
_mx("v", 128)
_mx("e", 512)
_mx("w", 512)
for _r in range(ROUNDS + 1):
    _mx("t%d" % _r, C)
for _r in range(ROUNDS):
    _mx("z%d" % _r, C)
    _mx("o%d" % _r, HALF)
    _mx("k%d" % _r, C)
for _n in BANKS:
    SCRATCH[_n] = ("psum", [128, 2048], "float32")

DMA_GROUPS = ["x", "xh", "u", "v", "w", "la", "lb", "ld", "le", "lf", "o"] + ["%s%d" % (n, r) for r in range(ROUNDS) for n in ("sw", "na", "n", "m", "mw", "tc")]
SEMAPHORES = ["cv", "cs", "ct", "cg", "snd"] + ["d" + n for n in DMA_GROUPS] + ["arr%d" % r for r in range(ROUNDS)]

TW, OF, PR, NW, MQ, OWN, NY, MO = [NG * k for k in range(8)]
EVEN, ODD = range(0, 8, 2), range(1, 8, 2)


def W(name, a=0, b=None, step=1, p0=0, p1=128, ind=None):
    return (name, a, SCRATCH[name][1][1] if b is None else b, step, p0, p1, ind)


def rank_program(g, core, T, topo):
    rank = T.rank_of(core)
    if rank is None:
        return

    queues = {"v": g.vector, "s": g.scalar, "t": g.tensor, "g": g, "y": g.sync}
    count, known, acc, snaps, waited = {}, {q: {} for q in queues}, {}, {}, {}

    def ap(v, bits=None):
        n, a, b, st, p0, p1, ind = v
        rows = slice(None) if (p0, p1) == (0, 128) else slice(p0, p1)
        t = T[n][rows, a:b] if st == 1 else T[n][rows, a:b:st]
        if bits is not None:
            t = t.bitcast(bits)
        return t if ind is None else t.indirect(ap(ind))

    def meets(r, s):
        return r[1] < s[2] and s[1] < r[2] and r[4] < s[5] and s[4] < r[5]

    def covers(r, s):
        return r[3] == 1 and r[1] <= s[1] and s[2] <= r[2] and r[4] <= s[4] and s[5] <= r[5]

    def whole(v):
        if SCRATCH[v[0]][0] == "psum":
            return (v[0], v[1] // 512 * 512, (v[2] + 511) // 512 * 512, 1, 0, 128, None)
        return v

    def phased(r, s):
        return r[3] > 1 and r[3] == s[3] and (r[1] - s[1]) % r[3] != 0

    def depend(q, reads, writes):
        need = {}
        for v, isw in [(whole(v), False) for v in reads] + [(whole(v), True) for v in writes]:
            for (rv, rw, rq, sem, val) in acc.get(v[0], []):
                if not (isw or rw) or not meets(v, rv) or phased(v, rv):
                    continue
                if isw and rq == q and q == "t":
                    continue
                need[sem] = max(need.get(sem, 0), count[sem] if sem[0] == "d" else val)
        k = known[q]
        for sem in sorted(need, key=lambda m: (m[0] == "c", m)):
            val = need[sem]
            if k.get(sem, 0) >= val:
                continue
            queues[q].wait_ge(T.sem[sem], val)
            k[sem] = val
            waited[sem] = max(waited.get(sem, 0), val)
            for s2, v2 in snaps.get((sem, val), {}).items():
                k[s2] = max(k.get(s2, 0), v2)

    def note(q, reads, writes, sem, inc):
        count[sem] = count.get(sem, 0) + inc
        val = count[sem]
        old = snaps.get((sem, val - inc), {}) if sem[0] == "d" else {}
        new = dict(known[q])
        for a, b in old.items():
            new[a] = max(new.get(a, 0), b)
        snaps[(sem, val)] = new
        for v in [whole(v) for v in writes]:
            lst = acc.setdefault(v[0], [])
            lst[:] = [r for r in lst if not covers(v, r[0])]
            lst.append((v, True, q, sem, val))
        for v in [whole(v) for v in reads]:
            acc.setdefault(v[0], []).append((v, False, q, sem, val))

    def op(q, call, reads, writes, sem=None, inc=1):
        reads = reads + [v[6] for v in reads + writes if v[6] is not None]
        sem = sem or "c" + q
        depend(q, reads, writes)
        call(queues[q]).then_inc(T.sem[sem], inc)
        note(q, reads, writes, sem, inc)

    def dma(group, out, in_, q="y"):
        o = ap(out) if isinstance(out, tuple) else out
        i = ap(in_) if isinstance(in_, tuple) else in_
        op(q, lambda e: e.dma_start(o, i), [in_] if isinstance(in_, tuple) else [], [out] if isinstance(out, tuple) else [], "d" + group, 16)

    def ts(out, in0, s1, s2, o0, o1=None):
        a1 = ap(s1) if isinstance(s1, tuple) else s1
        a2 = ap(s2) if isinstance(s2, tuple) else s2
        rd = [v for v in (in0, s1, s2) if isinstance(v, tuple)]
        if o1 is None:
            op("v", lambda e: e.tensor_scalar(ap(out), ap(in0), a1, None, o0), rd, [out])
        else:
            op("v", lambda e: e.tensor_scalar(ap(out), ap(in0), a1, a2, o0, o1), rd, [out])

    def tt(out, in0, in1, o):
        op("v", lambda e: e.tensor_tensor(ap(out), ap(in0), ap(in1), o), [in0, in1], [out])

    def cp(out, in_):
        op("v", lambda e: e.tensor_copy(ap(out), ap(in_)), [in_], [out])

    def act(out, in_, func=AF.Copy, **kw):
        op("s", lambda e: e.activation(ap(out), ap(in_), func, **kw), [in_], [out])

    def gcopy(out, in_):
        op("g", lambda e: e.affine_select(ap(out), ap(in_), [[0, C]], ALU.is_gt, 0.0, 1, 0), [in_], [out])

    def move(q, out, in_, scale=None):
        if q == "s":
            act(out, in_) if scale is None else act(out, in_, scale=scale)
        elif scale is None:
            cp(out, in_)
        else:
            ts(out, in_, scale, None, ALU.mult)

    def scan(out, d0, d1, first, o0, o1):
        op("v", lambda e: e.tensor_tensor_scan(ap(out), ap(d0), ap(d1), first, o0, o1), [d0, d1], [out])

    def iota(out, pattern, base, mult):
        kw = {} if SCRATCH[out[0]][2] == "int32" else {"allow_small_or_imprecise_dtypes": True}
        op("g", lambda e: e.iota(ap(out), pattern, base, mult, **kw), [], [out])

    def quant(name, in_, a=0, b=None):
        qo, so = W("q" + name, a, b), W("s" + name, a, b)
        op("v", lambda e: e.quantize_mx(ap(qo), ap(so), ap(in_)), [in_], [qo, so])

    def mm(out, ln, la, rn, ra, rb):
        l, ls, r, rs = W("q" + ln, la, la + 128), W("s" + ln, la, la + 128), W("q" + rn, ra, rb), W("s" + rn, ra, rb)
        op("t", lambda e: e.matmul_mx(ap(out), ap(l), ap(ls), ap(r), ap(rs), True, True), [l, ls, r, rs], [out])

    def bank(n, k, w, a=0):
        return W(n, 512 * k + a, 512 * k + a + w)

    def wl(k, n=1):
        return W("wl", k, k + n * NG)

    def raw(k, n=1):
        return W("lists", k, k + n * NG)

    def plane(n, b, a=0, w=C, ind=None):
        return W(n, b * C + a, b * C + a + w, ind=ind)

    def by(v, ind):
        return v[:6] + (ind,)

    def part(v, k):
        return v[:4] + (16 * (k % 8), 16 * (k % 8) + 16, None)

    def shift(grp, out, in_, to, by_, q="y"):
        for k in to:
            p = 16 * ((k + by_) % 8)
            dma(grp, part(out, k), part(in_, k + by_) if isinstance(in_, tuple) else in_[p:p + 16, :], q=q)

    def halves(out, window, offsets, cut=HALF):
        for q, a, b in (("v", cut, out[2] - out[1]), ("s", 0, cut)):
            move(q, W(out[0], out[1] + a, out[1] + b), by(window, W(offsets[0], offsets[1] + a // 16, offsets[1] + b // 16)))

    turn = [0]

    def slot():
        turn[0] += 1
        return C * (turn[0] % 6)

    def hold(row, pieces=None, at=None):
        n = row[2] - row[1]
        at = slot() if at is None else at
        for a, b in pieces or ((0, n),):
            scan(W("scn", at + a, at + b), W("hk", a, b), W(row[0], row[1] + a, row[1] + b), 0.0, ALU.mult, ALU.add)
        return W("scn", at + 15, at + n, 16)

    def places(out, held):
        ts(out, held, W("kinv"), float(HALF), ALU.mult, ALU.add)

    def wrap(out, row):
        places(out, hold(row))

    def mask_of(c):
        m = -1
        for s in STEPS:
            m &= topo.mask(c, T.cores[T.rank_of(c) ^ s])
        return m

    def load(grp, q, k, odd, even):
        shift(grp, raw(k), odd[0], ODD, odd[1], q)
        shift(grp, raw(k), even[0], EVEN, even[1], q)

    dma("u", W("ut"), T.u[:], q="s")
    dma("x", W("x0", 0, 4 * HALF), T.x[:, 0:4 * HALF])
    load("la", "s", TW, (T.nx, 0), (T.iv, -2))
    load("la", "y", OF, (T.nx, -1), (T.iv, -1))
    dma("xh", W("x0", 4 * HALF, 4 * C), T.x[:, 4 * HALF:4 * C])
    load("lb", "s", PR, (T.pr, 0), (T.pr, -2))
    load("lb", "y", NW, (T.iv, -1), (T.nx, -2))

    wr, ids, nrow, nw_, tn = W("wr", 0, C), W("wr", C, 2 * C), W("nb", HALF, HALF + C), W("wn", 12, 36), W("qb", C, 2 * C)
    iota(W("ip"), [[1, 1]], 0, 1)
    iota(W("ia"), [[16, NG]], 0, 0)
    iota(W("j16"), [[1, 16]], 0, 0)
    iota(W("uo", 0, 8), [[32, 4], [-80, 2]], 96, 0)
    op("v", lambda e: e.memset(ap(W("half")), 0.5), [], [W("half")])
    op("g", lambda e: e.affine_select(ap(W("et")), ap(W("half")), [[-1, 515]], ALU.is_equal, 0.0, 3, 4), [W("half")], [W("et")])
    ts(W("pm"), W("ip"), 15, None, ALU.bitwise_and)
    scan(ids, W("half", 0, C), W("half", 0, C), -HALF - 1.0, ALU.add, ALU.add)
    cp(W("pmf"), W("pm"))
    ts(W("wa"), W("ia"), W("pmf"), None, ALU.add)
    ts(W("ja"), W("j16"), W("pmf"), None, ALU.subtract)
    ts(W("rep"), W("ia"), 0.0, W("pmf"), ALU.mult, ALU.add)
    ts(W("uo", 8, 16), W("uo", 0, 8), 127, None, ALU.bitwise_and)
    ts(W("jb"), W("ja"), 1.0, BIG, ALU.is_equal, ALU.mult)
    ts(W("jc"), W("ja"), 0.0, None, ALU.is_gt)
    ts(W("kinv"), W("pmf"), 15.0, 1.0 / BIG, ALU.is_equal, ALU.max)
    cp(W("uof"), W("uo", 8, 16))
    tt(W("hk16"), W("jc"), W("jb"), ALU.max)
    ts(W("kin2"), W("pmf"), 15.0, 1.0 / BIG / BIG, ALU.is_equal, ALU.max)
    ts(raw(MQ), W("wa"), float(C), None, ALU.add)
    shift("ld", raw(MQ), T.iv, EVEN, -2)
    dma("ld", raw(OWN), T.iv[:])
    op("y", lambda e: e.dma_start(T.qw[:, 0:512].bitcast(dt.uint8), T.wc[:]), [], [W("qw")], "dw", 16)
    dma("w", W("sw"), T.ws[:])
    dma("v", W("vt"), T.v[:])
    act(W("hk"), W("hk16", ind=W("rep")))
    for o in (W("nas"), W("tm")):
        gcopy(o, ids)

    quant("u", W("ut"))
    qs, qd = W("qu", ind=W("uof")), W("qu2")
    op("v", lambda e: e.tensor_copy(ap(qd, dt.uint32), ap(qs, dt.uint32)), [qs], [qd])
    act(W("su2"), W("su", ind=W("uof")))
    quant("t0", W("x0", 0, 4 * HALF), 0, HALF)
    cp(wl(TW, 2), raw(TW, 2))
    act(W("tx"), by(ids, wl(TW)))
    for b in range(4):
        quant("e", W("et", 3 - b, 515 - b), 128 * b, 128 * b + 128)
        if b == 1:
            quant("t0", W("x0", 4 * HALF, 4 * C), HALF, C)
    cp(wl(PR, 2), raw(PR, 2))
    tt(W("e1"), raw(PR), W("wa"), ALU.subtract)
    tt(W("e2"), raw(PR), W("wa"), ALU.add)
    cp(W("ll"), W("wa"))
    ts(W("dlt"), W("e1"), 0.5, W("kin2"), ALU.mult, ALU.mult)
    ts(W("mid"), W("e2"), 0.5, None, ALU.mult)

    for r, step in enumerate(STEPS):
        last = r == ROUNDS - 1
        t, z, out, k = ["%s%d" % (n, r) for n in ("t", "z", "o", "k")]
        partner = T.cores[rank ^ step]
        pieces = PIECES if r else ((0, HALF), (HALF, C))
        for j, (a, b) in enumerate(pieces):
            mm(bank("psb", j, b - a), "u2", 0, t, a, b)
        for j, (a, b) in enumerate(pieces):
            if r > 0:
                ts(W("sg", a, b), bank("psb", j, b - a), 0.0, 0.5, ALU.is_gt, ALU.subtract)
            else:
                act(W("sg", a, b), bank("psb", j, b - a), AF.Sign, bias=-2.0 ** -100)
            if r == 0 and j == 0:
                act(tn, W("tx", ind=wl(OF)))
        for b in range(4):
            mm(bank("psa", b, C), "e", 128 * b, t, 0, C)
        if r > 0:
            own = hold(W("sg", 0, C), ((0, 256), (256, C)))
            halves(W("sg", C, 2 * C), W("sg", 0, C), wl(PR))
        else:
            at = slot()
            hold(W("sg", 0, C), ((0, HALF),), at)
            h1 = hold(tn)
            shift("le", tn, tn, EVEN, -1)
            halves(W("sg", C, 2 * C), W("sg", 0, C), wl(PR))
            places(W("wp"), h1)
            shift("lf", W("ll"), W("wp"), EVEN, 0)
            own = hold(W("sg", 0, C), ((HALF, C),), at)
            act(W("nw"), by(ids, wl(NW)))
        for b in range(2):
            act(plane("fp", b), bank("psa", b, C))
        if r > 0:
            tt(W("e1"), own, W("dlt"), ALU.mult)
        other = hold(W("sg", C, 2 * C))
        if r == 0:
            tt(W("e1"), own, W("dlt"), ALU.mult)
        else:
            h1 = hold(W("rl"))
        tt(W("e2"), other, W("e1"), ALU.mult)
        if r > 0:
            places(W("ll"), h1)
        tt(W("e3"), W("e2"), W("mid"), ALU.add)
        shift("sw%d" % r, W("e4"), W("e3"), EVEN, -1)
        shift("sw%d" % r, W("e4"), W("e3"), ODD[3:], 1)
        shift("sw%d" % r, W("e4"), W("e3"), ODD[:3], 1, "s")
        cp(W("ta"), W("e3"))
        cp(W("nti"), W("nw", ind=W("ta")))
        ts(W("tc"), W("ta"), float(C), None, ALU.add)
        shift("na%d" % r, W("nas"), W("nti"), EVEN, 2)
        act(W("qb", 0, C), by(tn, W("ta")))
        if r == 0:
            cp(wl(MQ), raw(MQ))
        cp(W("p4"), W("nti", ind=W("ll")))
        act(W("q2"), W("qb", ind=wl(MQ)))
        cp(plane("fp", 2, HALF, HALF), bank("psa", 2, HALF, HALF))
        cp(W("tb"), W("e4"))
        h1 = hold(W("p4"))
        halves(W("uu"), W("q2"), W("tb"), 224)
        places(W("wp"), h1)
        if r == 0:
            ts(W("dlt"), W("dlt"), 4.0, None, ALU.mult)
            cp(W("wm"), raw(OWN))
            cp(wl(MO), W("wa"))
        shift("tc%d" % r, W("tc"), W("ta"), EVEN, 2)
        shift("tc%d" % r, W("wm"), W("wp"), ODD, 1)
        halves(wr, W("uu"), W("wp"))
        act(plane("fp", 3), bank("psa", 3, C))
        act(plane("fp", 2, 0, HALF), bank("psa", 2, HALF))
        places(W("ww"), hold(wr, ((HALF, C), (0, HALF))))
        halves(W("nb", C, C + HALF), W("nas"), W("ww", 12, 24), 96)
        act(W("nb", HALF, C), W("nas", ind=W("ww", 0, 12)))
        lo, hi, lo2, hi2 = W("wn", 12, 24), W("wn", 24, 36), W("wn", 36, 48), W("wn", 0, 12)
        wrap(hi, W("nb", C, C + HALF))
        halves(W("nb", 0, HALF), nrow, hi, 96)
        for b in range(4):
            act(plane("an", b, HALF, HALF), plane("fp", b, ind=hi))
        h1, h2 = hold(W("nb", 0, HALF)), hold(W("nb", HALF, C))
        places(hi2, h1)
        places(lo, h2)
        for b in range(4):
            tt(W("zt", 4 * HALF + b, 4 * C, 4), plane("fp", b, ind=hi2), plane("an", b, HALF, HALF), ALU.add)
        act(W("nb", HALF + C, 2 * C), by(nrow, lo))
        for b in range(2):
            act(plane("an", b, 0, HALF), plane("fp", b, ind=lo))
        if not last:
            shift("n%d" % r, wl(NY), nw_, ODD, -1)
            shift("n%d" % r, wl(NY), nw_, EVEN, -2)
            shift("n%d" % r, W("nw"), nrow, EVEN, -2)
            gcopy(W("tx"), nrow)
            shift("n%d" % r, W("tx"), nrow, EVEN, -1)
        h1 = hold(W("nb", HALF + C, 2 * C))
        quant(out, W("zt", 4 * HALF, 4 * C))
        places(lo2, h1)
        rid, pid = topo.addr(partner)[:2]
        arr = "arr%d" % r
        depend("g", [W("q" + out), W("s" + out)], [])
        g.remote_dma(T["q" + z][:, HALF:C].bitcast(dt.uint8), T["q" + out][:, 0:HALF].bitcast(dt.uint8), T.sem[arr], T.sem.snd, pid, rid, mask_of(core))
        g.remote_dma(T["s" + z][:, HALF:C], T["s" + out][:, 0:HALF], T.sem[arr], T.sem.snd, pid, rid, mask_of(core))
        count["snd"] = count.get("snd", 0) + 2 * bin(mask_of(core)).count("1")
        count[arr] = 2 * bin(mask_of(partner)).count("1")
        for nm in ("q" + z, "s" + z):
            acc.setdefault(nm, []).append((W(nm, HALF, C), True, "far", arr, count[arr]))
        for b in (2, 3):
            act(plane("an", b, 0, HALF), plane("fp", b, ind=lo))
        for b in range(4):
            tt(W("zt", b, 4 * HALF, 4), plane("fp", b, ind=lo2), plane("an", b, 0, HALF), ALU.add)
        act(W("m1"), W("wr", ind=W("tc")))
        act(W("rm"), W("m1", ind=W("wm")))
        quant(z, W("zt", 0, 4 * HALF), 0, HALF)
        if r == 0:
            quant("v", W("vt"))

        def product(name, rhs, h):
            for b in range(4):
                mm(bank(BANKS[h], b, HALF), name, 128 * b, rhs, HALF * h, HALF * h + HALF)

        def scaled(q, h, b):
            move(q, W("ht", 4 * HALF * h + b, 4 * HALF * (h + 1), 4), bank(BANKS[h], b, HALF), 0.03125)

        def packed(h):
            quant(k, W("ht", 4 * HALF * h, 4 * HALF * (h + 1)), HALF * h, HALF * h + HALF)

        def added(h, planes):
            for b in planes:
                tt(plane("xn", b, HALF * h, HALF), bank(BANKS[h], b, HALF), plane("an", b, HALF * h, HALF), ALU.add)

        def inverse(held):
            places(W("wm"), held)
            if not last:
                g.sync.wait_ge(T.sem.snd, count["snd"])
                shift("m%d" % r, W("tm"), W("rm"), EVEN, -2)
                shift("m%d" % r, wl(MO), W("wm"), EVEN, -1)
                shift("mw%d" % r, W("nw"), W("rm"), ODD, -1)
                shift("mw%d" % r, wl(MQ), W("wm"), EVEN, -2)

        def beside():
            if not last:
                act(tn, W("tx", ind=wl(NY)))
            else:
                act(W("nlf"), nrow, AF.Identity, bias=float(HALF))
                op("y", lambda e: e.dma_start(T.nl[:], T.nlf[0:128:16, :]), [W("nlf")], [], "do", 16)

        product("w", z, 0)
        if r > 0:
            product("w", z, 1)
        for b in range(4):
            scaled("svsv"[b], 0, b)
        if r == 0:
            h1 = hold(W("rm"))
            packed(0)
            inverse(h1)
            beside()
            product("e", k, 0)
            added(0, range(4))
            product("w", z, 1)
            for b in range(4):
                scaled("svsv"[b], 1, b)
            packed(1)
            product("e", k, 1)
            added(1, range(4))
        else:
            scaled("s", 1, 0)
            h1 = hold(W("rm"))
            packed(0)
            inverse(h1)
            for q, b in (("v", 1), ("s", 2), ("v", 3)):
                scaled(q, 1, b)
            product("e", k, 0)
            packed(1)
            product("e", k, 1)
            beside()
            for h, planes in ((0, (0, 1, 2)), (1, (0, 1)), (0, (3,)), (1, (2, 3))):
                added(h, planes)
        for b in (0, 1):
            move("s", W("xt", b, 4 * C, 4), plane("xn", b, ind=W("wm")), 2.0)
        move("v", W("xt", 2, 4 * C, 4), plane("xn", 2, ind=W("wm")), 2.0)
        cut = 128 if r else 96
        move("s", W("xt", 3, 4 * cut, 4), plane("xn", 3, ind=W("wm", 0, cut // 16)), 2.0)
        move("v", W("xt", 4 * cut + 3, 4 * C, 4), plane("xn", 3, ind=W("wm", cut // 16, NG)), 2.0)
        if not last:
            act(W("rl"), W("tm", ind=wl(MO)))
        for a, b in PIECES:
            quant("t%d" % (r + 1), W("xt", 4 * a, 4 * b), a, b)

    f = "t%d" % ROUNDS
    for j, (a, b) in enumerate(PIECES):
        mm(bank("psb", j, b - a), "v", 0, f, a, b)
    op("s", lambda e: e.dma_start(T.oc[:], T["q" + f][:, 0:C].bitcast(dt.uint8)), [W("q" + f)], [], "do", 16)
    for q in range(4):
        op("y", lambda e: e.dma_start(T.osc[4 * q:4 * q + 4, :], T["s" + f][32 * q:32 * q + 4, 0:C]), [W("s" + f)], [], "do", 16)
    for j, (a, b) in enumerate(PIECES):
        move("vsv"[j], W("yo", a, b), bank("psb", j, b - a))
    dma("o", T.y[:], W("yo"))
    for sem in sorted(count, key=lambda m: (m == "do", m)):
        if waited.get(sem, 0) < count[sem]:
            g.wait_ge(T.sem[sem], count[sem])
